import numpy as np, ml_dtypes
CORES = [36,164,52,180,100,228,116,244]
N = 8
BF = ml_dtypes.bfloat16
W, L, C, SX, SL, STEPS = 2048, 512, 256, 8, 2, 4
def node(q, w):
    u = np.add.reduce(w[..., None] * q, axis=2) & (W - 1)
    return ((u * u >> 5) + 37 * u) & (W - 1)
def parts(rng):
    X = rng.integers(0, 256, (N, 8, 16, W))
    G = np.repeat(rng.integers(0, W, (1, 8, 16, L)), N, axis=0); cut = rng.integers(0, 22, (N, 8, 1, L))
    G = np.where((np.arange(16)[:, None] >= cut) | (rng.random(G.shape) < 0.05), rng.integers(0, W, G.shape), G)
    D = np.repeat(rng.integers(0, L, (1, 8, W)), N, axis=0); D = np.where(rng.random(D.shape) < 0.3, rng.integers(0, L, D.shape), D)
    q = rng.integers(0, 256, (N, 8, 16, C)); E = rng.integers(0, W, (N, 8, 16, C)); w = rng.integers(0, 256, (N, 8, 16))
    th = np.stack([rng.choice(np.array([500, 1100, 1300, 1450, 1600]), (N, 8)) + rng.integers(0, 60, (N, 8)), rng.integers(1000, 1650, (N, 8))], axis=2)
    return X, G, D, q, E, w, th
def pack(X, G, D, q, E, w, th):
    return {"xr": X.reshape(N, 128, W).astype(np.float32).astype(BF), "lg": G.reshape(N, 128, L).astype(np.int32), "dr": D.astype(np.int32), "qd": q.reshape(N, 128, C).astype(np.float32).astype(BF),
            "e0": E.reshape(N, 128, C).astype(np.int32), "wt": w.reshape(N, 128, 1).astype(np.float32).astype(BF), "th": th.astype(np.int32)}
def setup_inputs(rng):
    return pack(*parts(rng))
def setup_inputs_spread(rng):
    X, G, D, q, E, w, th = parts(rng)
    X = np.minimum((np.exp2(8 * rng.random((N, 8, 1, W))) * (0.25 + rng.random(X.shape))).astype(np.int64), 255)
    q = np.minimum((np.exp2(8 * rng.random((N, 8, 1, C))) * (0.25 + rng.random(q.shape))).astype(np.int64), 255)
    w = np.minimum(np.exp2(8 * rng.random(w.shape)).astype(np.int64), 255); th = np.minimum(np.exp2(5 + 7 * rng.random(th.shape)).astype(np.int64), 4079)
    G = np.where(rng.random(G.shape) < 0.5, G, (W * rng.random(G.shape) ** 3).astype(np.int64)); D = np.where(rng.random(D.shape) < 0.5, D, (L * rng.random(D.shape) ** 3).astype(np.int64))
    E = (W * rng.random(E.shape) ** 2).astype(np.int64)
    return pack(X, G, D, q, E, w, th)
def ends_of(rng, shape, hi, share):
    return np.where(rng.random(shape) < share, hi * rng.integers(0, 2, shape), rng.integers(0, hi + 1, shape))
def setup_inputs_ends(rng):
    kx, kq = rng.random((N, 8, 1, W)), rng.random((N, 8, 1, C))
    X = np.where(kx < 0.2, 0, np.where(kx < 0.4, 255, 255 * rng.integers(0, 2, (N, 8, 16, W)))); q = np.where(kq < 0.2, 0, np.where(kq < 0.4, 255, 255 * rng.integers(0, 2, (N, 8, 16, C))))
    X[:, ::2, :, 0] = 255; X[:, ::2, :, W - 1] = 0; X[:, 1::2, :, 0] = 0; X[:, 1::2, :, W - 1] = 255
    G = ends_of(rng, (N, 8, 16, L), W - 1, 0.7); D = ends_of(rng, (N, 8, W), L - 1, 0.7); E = ends_of(rng, (N, 8, 16, C), W - 1, 0.7)
    free = np.argsort(rng.random((N, 8, 16)), axis=2) < 4
    w = np.where(free, rng.integers(0, 256, (N, 8, 16)), 255 * rng.integers(0, 2, (N, 8, 16))); w[:, 0, 0] = 0; w[:, 0, 1] = 255; w[N - 1, 7] = 255
    r, g = np.arange(N)[:, None], np.arange(8)[None, :]
    th = np.stack([np.where((r + g) % 2 == 0, 4079, 0), np.where((g % 2 == 1) & (g < 7), rng.integers(1000, 3000, (N, 8)), np.where((r + (g >> 1)) % 2 == 0, 0, 4079))], axis=2); th[N - 1, 7] = 4079
    q[:, 7, :, C - 1] = 255; q[:, 6, :, C - 1] = 0; q[N - 1, 7][:, [0, 1, C - 1]] = 255
    n = node(q, w)
    for a in range(N):
        D[a, 7, n[a, 7, C - 1]] = L - 1; D[(a + 1) % N, 7, n[a, 7, C - 1]] = L - 1
        G[a, 7, :, L - 1] = (W - 1) * ((a + 1) % 2)
    G[N - 1, 7, :, L - 1] = 0; G[0, 7, :, L - 1] = W - 1; G[0, 7, 15, L - 1] = 0
    return pack(X, G, D, q, E, w, th)
def setup_inputs_corners(rng):
    X, G, D, q, E, w, th = parts(rng)
    m = rng.integers(3, 30, (N, 8)); th[:, :, 0] = 32 * m - 1; th[:, :, 1] = 16 * m; m = m[:, :, None, None]; one = np.eye(16, dtype=np.int64)
    w[..., 0] = 0; w[..., 15] = 255
    nm = SX * np.argsort(rng.random((8, C)), axis=1)[:, :, None] + np.arange(5)
    r0 = rng.integers(4, 90, (N, 8, C, 16)); r2 = r0 + 2 * m
    rec = np.stack([r0, r2 - one[0], r2, r0 - one[1] - one[2], r2 + one[1] + one[2]], axis=3)
    kd = rng.choice(np.array([0, 1, 8, 14, 15, 16]), (N, 8, C)); ks = np.minimum(kd, 15); side = rng.integers(-1, 2, (N, 8, C))
    d = r0 + m + side[..., None] * one[0]
    q = np.ascontiguousarray((d + np.where(kd[..., None] == 0, 0, r0)).transpose(0, 1, 3, 2))
    st = np.maximum(ks + 1, rng.choice(np.array([0, 5, 15, 16]), (N, 8, C)))[..., None]; kk = np.arange(16)
    hj = np.where(kk < st, 0, 3); fj = np.where(kk < kd[..., None], rng.integers(0, 2, (N, 8, C, 16)), np.where(kk < st, 2, 4))
    pal = np.broadcast_to(nm, (N, 8, C, 5)); hn = np.take_along_axis(pal, hj, 3); fn = np.take_along_axis(pal, fj, 3)
    n = node(q, w); col = SL * np.arange(C)
    for a in range(N):
        b = (a + 1) % N
        for g in range(8):
            X[a, g][:, nm[g].reshape(-1)] = rec[a, g].reshape(-1, 16).T
            G[a, g][:, col] = hn[a, g].T; G[b, g][:, col + 1] = fn[a, g].T
            D[b, g, n[a, g]] = col + 1
    for a in range(N):
        for g in range(8): D[a, g, n[a, g]] = col
    return pack(X, G, D, q, E, w, th)
def setup_inputs_crowd(rng):
    X, G, D, q, E, w, th = parts(rng)
    q[:3] = rng.integers(200, 256, q[:3].shape); w[:, 1:3, 0] = 1; w[:, 6] = 0
    q[:, 0:3] = q[:, 0:3, :, :1].copy(); q[:, 1, 0, C - 1] ^= 1; q[:, 2, 0, 0] ^= 1
    q[:, 3, :, 0::2] = q[:, 3, :, :1].copy(); q[:, 3, :, 1::2] = q[:, 3, :, 1:2].copy()
    D[:, 4] = rng.choice(np.array([0, L - 1, L // 2]), (N, W)); G[:, 5, 1:] = rng.choice(np.array([0, 1, W - 1]), (N, 15, L))
    nm = 2 * rng.permutation(W >> 1)[:N] + 1
    for a in range(N): G[a, :, 0, :] = nm[a]
    for a in range(2): X[a, :, :, nm[a]] = 0; X[a, :, :, nm[a + 1]] = 255; th[a, :, 0] = 0
    X[2, :, :, nm[2]] = 255; X[2, :, :, nm[3]] = 0; th[2, :, 0] = 0
    q[1, 7, :, C - 1] = 0
    v = np.arange(1, 4081); u = (255 * v) & (W - 1); k = W - 1 - (((u * u >> 5) + 37 * u) & (W - 1))
    j = int(rng.choice(np.flatnonzero((k >= 1) & (k <= 7 * (C - 1))))); v, u, k = int(v[j]), int(u[j]), int(k[j])
    X[3][:, :, nm] = 0; X[3][:, :, nm[3]] = 255; th[3] = 0; G[3, :, 1, :] = nm[2]
    w[3] = 0; w[3, 7] = rng.permutation(v // 16 + (np.arange(16) < v % 16))
    lose = rng.permutation(7 * (C - 1))[:k]; q[3] = 255; q[3, lose // (C - 1), :, 1 + lose % (C - 1)] = 0
    D[3, :7] |= 1; D[3, 7, W - 1] = SL * int(rng.integers(0, C)) + ((u & (SL - 1)) ^ 1); E[3, 7, :, 0] = nm[3]
    return pack(X, G, D, q, E, w, th)
def setup_inputs_brink(rng):
    X, G, D, q, E, w, th = parts(rng); nm = rng.permutation(W)[:6]
    for a in range(N):
        b = a % 2; own, oth = nm[b], nm[1 - b]
        for g in (0, 7):
            G[a, g, 0, :] = own; X[a, g, :, own] = 0; X[a, g, :, oth] = 0; X[a, g, int(rng.integers(0, 16)), oth] = 1
            q[a, g, :, 1::2] = 255; th[a, g, 0] = 0
        G[a, 2, 0, :] = own; G[a, 2, 3, :] = nm[2 + b]; X[a, 2, :, own] = 0; X[a, 2, :, oth] = 255; X[a, 2, int(rng.integers(0, 16)), oth] = 254
        X[a, 2, :, nm[2 + b]] = 255; X[a, 2, :, nm[3 - b]] = 0; th[a, 2, 0] = 4079
        G[a, 4, 0, :] = own; G[a, 4, 1, :] = nm[4]; G[a, 4, 2, :] = nm[5]; X[a, 4, :, own] = 200; X[a, 4, :, oth] = 100
        X[a, 4, :, nm[4]] = 0; X[a, 4, int(rng.integers(0, 16)), nm[4]] = 1; X[a, 4, :, nm[5]] = 0
        q[a, 4, :, 1::2] = 255; th[a, 4, 0] = 0; th[a, 4, 1] = 4079
    for v in (X, G, D, q, E, w, th): v[2] = v[0]; v[3] = v[1]
    return pack(X, G, D, q, E, w, th)
def check_inputs(d):
    bad = []
    for k, hi in (("xr", 255), ("lg", W - 1), ("dr", L - 1), ("qd", 255), ("e0", W - 1), ("wt", 255), ("th", 4079)):
        v = np.asarray(d[k]).astype(np.float64)
        if not (np.min(v) >= 0 and np.max(v) <= hi): bad.append("range of " + k)
        elif np.any(v != np.floor(v)): bad.append("whole numbers of " + k)
    return bad
def column(logs, book, n):
    return np.take_along_axis(logs, np.take_along_axis(book, n, 1)[:, None, :], 2)
def records(X, names):
    return np.take_along_axis(X, np.ascontiguousarray(names.transpose(0, 2, 1)).reshape(8, 1, C * 16), 2).reshape(8, 16, C, 16)
def reference(xr, lg, dr, qd, e0, wt, th):
    X = xr.astype(np.float32).astype(np.int32).reshape(N, 8, 16, W); G = lg.astype(np.int32).reshape(N, 8, 16, L); D = dr.astype(np.int64).reshape(N, 8, W)
    q = qd.astype(np.float32).astype(np.int32).reshape(N, 8, 16, C); E = e0.astype(np.int32).reshape(N, 8, 16, C)
    w = wt.astype(np.float32).astype(np.int32).reshape(N, 8, 16, 1); h = th.astype(np.int64).reshape(N, 8, 2); A = np.zeros(N, np.int64)
    kk = np.arange(16); i = np.arange(C)
    for t in range(STEPS):
        u = np.add.reduce(w * q, axis=2).astype(np.int64) & (W - 1)
        n = ((u * u >> 5) + 37 * u + A[:, None, None]) & (W - 1)
        own, other = [], []
        for r in range(N):
            f = (r + 1 + t % (N - 1)) % N
            own.append(column(G[r], D[r], n[r])); other.append(column(G[f], D[f], n[r]))
        for r in range(N):
            P, B = own[r], other[r]
            x = records(X[r], P); y = records(X[r], B)
            apart = np.add.reduce(np.abs(x - y), axis=1) > h[r, :, 0][:, None, None]
            ks = np.where(np.any(apart, axis=2), np.argmax(apart, axis=2), 15)
            M = np.max(np.where(kk < ks[:, None, :, None], x, 0), axis=3)
            d = np.abs(q[r] - M)
            xs = np.take_along_axis(x, ks[:, None, :, None], 3)[..., 0]; ys = np.take_along_axis(y, ks[:, None, :, None], 3)[..., 0]
            lost = np.add.reduce(np.abs(ys - d), axis=1) < np.add.reduce(np.abs(xs - d), axis=1)
            z = np.where(lost[:, None, :, None], y, x)
            over = (np.add.reduce(np.abs(z - d[..., None]), axis=1) > h[r, :, 1][:, None, None]) & (kk > ks[:, :, None])
            e = np.where(np.any(over, axis=2), np.argmax(over, axis=2), 16)
            last = np.take_along_axis(z, (e - 1)[:, None, :, None], 3)[..., 0]
            E[r] = np.where(kk[None, :, None] < e[:, None, :], np.where((kk[None, :, None] >= ks[:, None, :]) & lost[:, None, :], B, P), E[r])
            cl = SL * i + (u[r] & (SL - 1)); cx = (SX * i + (u[r] & (SX - 1)))[:, None, :]
            np.put_along_axis(G[r], cl[:, None, :], E[r], 2)
            old = np.take_along_axis(X[r], cx, 2); np.put_along_axis(X[r], cx, (old + d) >> 1, 2)
            if t + 1 < STEPS:
                for g in range(8):
                    v, first = np.unique(n[r, g], return_index=True)
                    D[r, g, v] = cl[g, first]
            q[r] = (d + last) >> 1; A[r] = np.count_nonzero(lost)
    return {"yl": G.reshape(N, 128, L).astype(np.float32), "yx": X.reshape(N, 128, W).astype(np.float32).astype(BF), "yq": q.reshape(N, 128, C).astype(np.float32).astype(BF)}

@@ -1,0 +1,792 @@
+import numpy as np
+from concourse.bass import DstId, RemoteDMATransfer
+from concourse.mybir import dt, AluOpType, AxisListType, ActivationFunctionType
+
+N, STEPS, C = 8, 4, 256
+F16 = "float16"
+CFG = {
+    "CH": [64, 64, 64, 64],
+    "NG": [0, 3, 4],
+    "SUB": 32,
+    "ABS": [1, 0, 0, 0],
+    "PG": [0, 1, 3, 4],
+    "LS": 1,
+    "ZP": 1,
+    "SC": 1024,
+    "oc": 1,
+    "P2": [0, 0, 0, 1],
+    "AV": [0, 0, 1, 1],
+    "YS": [0, 1, 0, 0],
+    "EP": 1,
+    "MV": 0,
+}
+CFG.update({'CH': [96, 96, 64], 'NG': [0, 1, 3], 'SUB': 32, 'ABS': [1, 1, 0], 'PG': [0, 1, 3], 'LS': 0, 'ZP': 2, 'SC': 1024, 'oc': 1,
+            'P2': [0, 0, 0], 'AV': [0, 0, 0], 'YS': [0, 0, 0], 'EP': 0, 'MV': 0})
+BIAS = {'~SVc192n': -4000, 'Sd96c1': -1000, 'VbI0i': -4000, 'Sdm192c2': 3500, 'c2c': -1000, 'Vmq192c2': -4000, 'Vt10n': 4000, 'Pp00c1': 1000, 'GGf0c0': 4000, 'Szb3072c2': -4000, 'VDg20n': 1000, 'Pp10c2': -2000, 'VDw0n': -2000, 'Vpm2560c1': 500, 'VG0i': -1000, '~Srl3584c2': -2000, 'Vuc0n': -4000, '~Sxb3120c2': 1500, 'Slts96c1': -1000, 'c2d': 4500, 'Sxb2080c1': -500, 'c0a': 1000, 'Vu00n': 1000, 'Szb0c0': -4000, 'Saz2592c1': -1000, 'VeL12c2': -4000, '~Szb1024c0': 1000, 'Ssg20c0': -2000, 'Vnh6n': -2000, '~Sxs192c2': -4000, '~Szb1536c1': 4000, 'Sd0c0': 4000, 'Vnh16n': -2000, 'nd': 1000, 'VG192c1': -500, 'Vx20x': 500, 'Vpm1024c0': 500, 'VE0i': 500, 'Sd192c2': 500, 'SIn0i': -1000, 'Vpm3072c2': -4000, 'Vdl2080c1': 2000, 'Vcf4i': 1000, 'VWh0i': -1000, 'Sm010c0': 4000, 'Pp50c0': 500, 'Vkm0i': -500, 'Srl3584c2': 1000, 'Pp40n': 500, 'c0d': -1000, 'SVc96n': 4000}
+EVEN = 2560.0
+BIG = 8192.0
+PAD = 16
+
+SCRATCH = {
+    "X": ("sbuf", [128, 2048], "bfloat16"), "G": ("sbuf", [128, 512], "float32"), "Gi": ("sbuf", [128, 512], "int32"),
+    "Gf": ("sbuf", [128, 1536], "float32"), "G0": ("sbuf", [128, 512], "int32"), "X2": ("sbuf", [128, 2048], "bfloat16"),
+    "BOw": ("sbuf", [128, 128], F16), "cn": ("sbuf", [128, 16], F16), "In16": ("sbuf", [128, 128], F16),
+    "ds": ("sbuf", [128, 256], "bfloat16"), "al": ("sbuf", [128, 512], "bfloat16"), "Dg2": ("sbuf", [128, 256], F16),
+    "Dw": ("sbuf", [128, 2064], "int32"), "Ds": ("sbuf", [128, 128], "int32"), "Dl": ("sbuf", [128, 512], "int32"),
+    "Tv": ("sbuf", [128, 2048], "float32"),
+    "xb": ("sbuf", [128, 4096 + 8 * PAD], "bfloat16"), "dl": ("sbuf", [128, 4096 + 8 * PAD], "bfloat16"),
+    "Zr": ("sbuf", [128, 128], "bfloat16"), "I4n": ("sbuf", [128, 128], "bfloat16"), "Wl": ("sbuf", [128, 144], "bfloat16"), "eD": ("sbuf", [128, 16], "uint16"),
+    "vq": ("sbuf", [128, 256], "float32"), "Ef": ("sbuf", [128, 384], F16), "clf": ("sbuf", [128, 48], "uint16"),
+    "rl": ("sbuf", [128, 4096], "bfloat16"), "pm": ("sbuf", [128, 4096], "bfloat16"),
+    "zb": ("sbuf", [128, 4096], "bfloat16"), "az": ("sbuf", [128, 4096], "bfloat16"),
+    "q": ("sbuf", [128, 256], "bfloat16"), "q2": ("sbuf", [128, 256], F16),
+    "Ei": ("sbuf", [128, 256], "int32"), "E": ("sbuf", [128, 256], F16),
+    "wc": ("sbuf", [128, 16], "bfloat16"), "thi": ("sbuf", [128, 4], "int32"), "thf": ("sbuf", [128, 4], "float32"),
+    "ci": ("sbuf", [128, 8], "int32"), "cf": ("sbuf", [128, 16], "float32"), "bs": ("sbuf", [128, 4], "float32"),
+    "Xr": ("sbuf", [128, 144], "float32"), "X16": ("sbuf", [128, 128], "float32"), "Lr": ("sbuf", [128, 256], "bfloat16"),
+    "ai": ("sbuf", [128, 48], "float32"), "bI": ("sbuf", [128, 32], "int32"), "bL": ("sbuf", [128, 16], "bfloat16"),
+    "W": ("sbuf", [128, 144], "bfloat16"), "W2": ("sbuf", [128, 144], "bfloat16"), "Wn": ("sbuf", [128, 144], "bfloat16"),
+    "Ww": ("sbuf", [128, 144], "bfloat16"), "Wh": ("sbuf", [128, 144], F16),
+    "WD0": ("sbuf", [128, 144], F16), "WD1": ("sbuf", [128, 144], F16),
+    "I": ("sbuf", [128, 128], "bfloat16"), "In": ("sbuf", [128, 128], "bfloat16"), "I16": ("sbuf", [128, 128], F16),
+    "I4": ("sbuf", [128, 128], "bfloat16"), "IB": ("sbuf", [128, 128], "bfloat16"), "Sh": ("sbuf", [128, 128], "bfloat16"),
+    "BO": ("sbuf", [128, 128], "bfloat16"), "BO2": ("sbuf", [128, 128], "bfloat16"), "BOn": ("sbuf", [128, 128], "bfloat16"),
+    "BOn2": ("sbuf", [128, 128], "bfloat16"), "Tri": ("sbuf", [128, 128], "bfloat16"), "W15": ("sbuf", [128, 128], "float32"),
+    "E8": ("sbuf", [128, 128], "float32"), "Cm": ("sbuf", [128, 256], "bfloat16"),
+    "km": ("sbuf", [128, 1024], "bfloat16"),
+    "u0": ("sbuf", [128, 16], "int32"), "u": ("sbuf", [128, 16], "int32"), "t1": ("sbuf", [128, 16], "int32"),
+    "t2": ("sbuf", [128, 16], "int32"), "t3": ("sbuf", [128, 16], "int32"), "nI": ("sbuf", [128, 16], "int32"),
+    "ub": ("sbuf", [128, 32], "int32"), "uc": ("sbuf", [128, 32], "int32"),
+    "n16": ("sbuf", [128, 32], "uint16"), "cx16": ("sbuf", [128, 64], "uint16"), "nh": ("sbuf", [128, 32], F16),
+    "cL": ("sbuf", [128, 32], "uint16"), "nd": ("sbuf", [128, 32], "uint16"),
+    "sL": ("sbuf", [128, 16], "uint16"), "eL": ("sbuf", [128, 16], "uint16"),
+    "Dg": ("sbuf", [128, 256], F16), "nr": ("sbuf", [128, 256], "float32"), "Vc": ("sbuf", [128, 256], "float32"),
+    "eq": ("sbuf", [128, 256], "bfloat16"),
+    "P16": ("sbuf", [128, 256], "uint16"), "B16": ("sbuf", [128, 256], "uint16"), "Z16": ("sbuf", [128, 256], "uint16"),
+    "Pf": ("sbuf", [128, 256], F16), "Bf": ("sbuf", [128, 256], F16), "Ih16": ("sbuf", [128, 128], F16),
+    "tz": ("sbuf", [128, 256], F16), "df": ("sbuf", [128, 256], F16), "te": ("sbuf", [128, 256], F16),
+    "sg": ("sbuf", [128, 256], "bfloat16"), "lts": ("sbuf", [128, 256], "bfloat16"), "sg2": ("sbuf", [128, 512], "bfloat16"),
+    "lte": ("sbuf", [128, 256], "bfloat16"), "mq": ("sbuf", [128, 256], "bfloat16"), "d": ("sbuf", [128, 256], "bfloat16"),
+    "dm": ("sbuf", [128, 256], "float32"), "xs": ("sbuf", [128, 256], "bfloat16"), "ys": ("sbuf", [128, 256], "bfloat16"),
+    "mx": ("sbuf", [128, 256], "bfloat16"), "my": ("sbuf", [128, 256], "bfloat16"), "m01": ("sbuf", [128, 256], "bfloat16"),
+    "jk": ("sbuf", [128, 256], "bfloat16"), "ac": ("sbuf", [128, 4], "float32"), "Ac": ("sbuf", [128, 4], "float32"),
+    "xo": ("sbuf", [128, 256], F16), "x2": ("sbuf", [128, 256], "bfloat16"),
+}
+for _b in range(8):
+    SCRATCH["p%d" % _b] = ("psum", [128, 512], "float32")
+NDS = 70
+SEMAPHORES = ["V", "S", "P", "G"] + ["m%d" % i for i in range(NDS)] + ["a%d" % i for i in range(28)]
+IO = {"xr": 2, "lg": 4, "dr": 4, "qd": 2, "e0": 4, "wt": 2, "th": 4, "yl": 4, "yx": 2, "yq": 2}
+SIZE = {"float32": 4, "int32": 4, "bfloat16": 2, "float16": 2, "uint16": 2}
+COST = {"cyc": 1.0, "pe": 0.5, "fix": 60.0, "wake": 80.0, "gat": 1.56, "sca": 3.8, "tt2": 1.0, "dma": 2000.0, "rem": 2500.0,
+        "issue": 600.0, "lbw": 150.0, "rbw": 50.0}
+A_ = AluOpType
+F_ = ActivationFunctionType
+
+
+def ap(name, c0=0, c1=None, step=1, rows=None):
+    if c1 is None:
+        c1 = SCRATCH[name][1][1] if name in SCRATCH else -1
+    return ("ap", name, c0, c1, step, rows)
+
+
+def ind(win, off):
+    return ("ind", win, off)
+
+
+def is_ap(a):
+    return isinstance(a, tuple) and len(a) > 0 and a[0] in ("ap", "ind")
+
+
+def count(a):
+    if a[0] == "ind":
+        return 16 * count(a[2])
+    return (a[3] - a[2] + a[4] - 1) // a[4]
+
+
+def width(a):
+    n = a[1][1] if a[0] == "ind" else a[1]
+    return SIZE[SCRATCH[n][2]] if n in SCRATCH else IO[n]
+
+
+def in_psum(a):
+    return a[0] == "ap" and a[1] in SCRATCH and SCRATCH[a[1]][0] == "psum"
+
+
+def regions(a):
+    if a[1] not in SCRATCH:
+        return []
+    if in_psum(a):
+        return [(a[1], 0, 512)]
+    if a[1] == "Dw":
+        return [("Dw%d" % r, a[2], a[3]) for r in (0, 1) if a[5] is None or a[5][0] == r]
+    return [(a[1], a[2], a[3])]
+
+
+def real(T, a):
+    if a[0] == "ind":
+        return real(T, a[1]).indirect(real(T, a[2]))
+    t = T[a[1]]
+    if a[3] < 0:
+        return t[:]
+    r = slice(None) if a[5] is None else slice(*a[5])
+    return t[r, a[2]:a[3]] if a[4] == 1 else t[r, a[2]:a[3]:a[4]]
+
+
+def build(cfg, K):
+    ops = []
+    where = ["i", "a"]
+
+    def add(eng, calls, occ, lat, kind="c", extra=None):
+        rd, wr = [], []
+        for (m, args, kw) in calls:
+            for i, a in enumerate(list(args) + list(kw.values())):
+                if not is_ap(a):
+                    continue
+                out = i == 0 or (i >= len(args) and a is kw.get("accum_out"))
+                if a[0] == "ind":
+                    rd.extend(regions(a[2]))
+                    a = a[1]
+                (wr if out or in_psum(a) else rd).extend(regions(a))
+        a = extra[0] if kind == "send" else calls[0][1][0]
+        a = a[1] if a[0] == "ind" else a
+        key = "%s%s%d%s" % (eng, a[1], a[2] % 512 if a[1] == "Gf" else a[2], where[0])
+        ops.append({"eng": eng, "calls": calls, "occ": occ, "lat": lat, "kind": kind, "rd": rd, "wr": wr, "x": extra, "key": key,
+                    "grp": where[0] + where[1]})
+
+    def ecost(m, args):
+        aps = [a for a in args if is_ap(a) and (a[0] == "ind" or count(a) > 1 or a is args[0])]
+        n = max(count(a) if a[0] == "ind" or a is args[0] else 0 for a in aps)
+        if aps[0][0] == "ind":
+            c = n * K["sca"]
+        elif any(a[0] == "ind" for a in aps):
+            c = n * K["gat"]
+        else:
+            two = all(width(a) == 2 for a in aps)
+            if m == "tensor_tensor":
+                c = n * (1.0 if any(in_psum(a) for a in aps[1:]) else (K["tt2"] if two else 2.0))
+            elif m == "activation":
+                c = n
+            else:
+                c = n * (0.5 if two else 1.0)
+            c = max(c, 64 - K["fix"])
+        return K["fix"] + c * K["cyc"]
+
+    def V(m, *args):
+        c = ecost(m, args)
+        add("V", [(m, args, {})], c, c)
+
+    def tt(o, a, b, op):
+        V("tensor_tensor", o, a, b, op)
+
+    def ts(o, a, s1, op0, s2=None, op1=None):
+        if op1 is None:
+            V("tensor_scalar", o, a, s1, None, op0)
+        else:
+            V("tensor_scalar", o, a, s1, s2, op0, op1)
+
+    def cp(o, a):
+        V("tensor_copy", o, a)
+
+    def act(o, a, f, **kw):
+        c = ecost("activation", (o, a))
+        add("S", [("activation", (o, a, f), kw)], c, c)
+
+    def either(o, a, relu=False):
+        act(o, a, F_.Relu if relu else F_.Copy)
+        call = ("tensor_scalar", (o, a, 0.0, None, A_.max), {}) if relu else ("tensor_copy", (o, a), {})
+        c = ecost(call[0], call[1])
+        ops[-1]["alt"] = {"eng": "V", "calls": [call], "occ": c, "lat": c}
+
+    def mm(group, start=True, stop=True):
+        calls, c = [], 0.0
+        for i, e in enumerate(group):
+            if e is None:
+                continue
+            o, l, r = e
+            calls.append(("matmul", (o, l, r, start if i == 0 else group[i - 1] is None,
+                                     stop if i == len(group) - 1 else group[i + 1] is None), {}))
+            c += max(min(64, count(l)), count(r)) * (4 if width(r) == 4 else 1) * K["pe"]
+        add("P", calls, c, c + K["fix"])
+
+    def iota(o, pat, base, cm):
+        kw = {} if SCRATCH[o[1]][2] == "int32" else {"allow_small_or_imprecise_dtypes": True}
+        c = 130 + 2 * count(o) * K["cyc"]
+        add("G", [("iota", (o, pat, base, cm), kw)], c, c)
+
+    def dma(o, i, nbytes, eng="Y"):
+        add(eng, [("dma_start", (o, i), {})], 100.0, K["dma"] + nbytes / K["lbw"], "dma")
+
+    def send(o, i, back):
+        nb = 128 * count(i) * width(i)
+        add("G", [("remote", (None, i), {})], K["issue"], K["issue"] + 1000 + nb / K["rbw"], "send", (o, back))
+        ops.append({"eng": None, "calls": [], "occ": 0.0, "lat": K["rem"] + nb / K["rbw"], "kind": "arr", "rd": [],
+                    "wr": regions(o), "x": len(ops) - 1})
+
+    def sel(name, k):
+        return ap(name, 15 - k, 143 - k)
+
+    def col(name, j):
+        return ap(name, j, j + 1)
+
+    CH = cfg["CH"]
+    J = [sum(CH[:i]) for i in range(len(CH) + 1)]
+    dma(ap("q"), ap("qd"), 65536)
+    dma(col("wc", 0), ap("wt"), 4096, "S")
+    dma(ap("Gi", 0, 256), ap("lg", 0, 256), 131072, "S")
+    dma(ap("Gi", 256, 512), ap("lg", 256, 512), 131072, "S")
+    dma(ap("Ds"), ap("dr"), 65536)
+    dma(ap("thi", 0, 2, 1, (0, 8)), ap("th"), 1024, "S")
+    for m0 in range(0, 2064, 688):
+        V("memset", ap("Dw", m0, m0 + 688), 0)
+    dma(ap("Dw", 0, 2048, 1, (0, 128, 16)), ap("dr"), 65536)
+    dma(ap("X"), ap("xr"), 524288)
+    dma(ap("Ei"), ap("e0"), 131072, "S")
+    iota(col("ci", 0), [[0, 1]], 0, 1)
+    iota(ap("Xr"), [[1, 144]], 0, 0)
+    ts(col("ci", 1), col("ci", 0), 112, A_.bitwise_and)
+    ts(col("ci", 2), col("ci", 0), 15, A_.bitwise_and)
+    cp(ap("cf", 0, 3), ap("ci", 0, 3))
+    pc, gc, kc = col("cf", 0), col("cf", 1), col("cf", 2)
+    ts(ap("W"), ap("Xr"), gc, A_.subtract, 15.0, A_.is_equal)
+    ts(ap("Ww"), ap("W"), col("wc", 0), A_.mult)
+    cp(ap("G"), ap("Gi"))
+    send(ap("Dl", 0, 128), ap("Ds"), 1)
+    send(ap("G0", 0, 256), ap("Gi", 0, 256), 1)
+    send(ap("G0", 256, 512), ap("Gi", 256, 512), 1)
+    ts(col("cf", 3), kc, 0.0, A_.is_equal)
+    ts(col("cf", 4), kc, 1.0, A_.is_equal)
+    ts(col("cf", 5), kc, 15.0, A_.is_equal)
+    ts(col("cf", 6), kc, 15.0, A_.not_equal)
+    ts(col("cf", 7), kc, -1.0, A_.mult)
+    ts(col("cf", 8), kc, 2048.0, A_.add)
+    ts(col("cf", 9), pc, 16.0, A_.mult)
+    ts(col("cf", 10), col("cf", 3), -BIG, A_.mult, -0.5, A_.add)
+    ts(ap("WD0"), ap("W"), col("cf", 3), A_.mult)
+    ts(ap("WD1"), ap("W"), col("cf", 4), A_.mult)
+    ts(ap("Wh"), ap("Ww"), 0.5, A_.mult)
+    for (o, s, f) in (("W2", "W", 2.0), ("Wn", "W", -1.0)):
+        act(ap(o), ap(s), F_.Identity, scale=f)
+    x128 = ap("Xr", 0, 128)
+    ts(ap("I"), x128, pc, A_.is_equal)
+    cp(ap("I16"), ap("I"))
+    iota(ap("X16"), [[16, 8], [0, 16]], 0, 0)
+    ts(ap("BO"), ap("X16"), gc, A_.is_equal)
+    for (o, s, f) in (("In", "I", -1.0), ("I4", "I", 4096.0), ("IB", "I", -BIG), ("BO2", "BO", 2.0), ("BOn", "BO", -1.0),
+                      ("BOn2", "BO", -2.0)):
+        act(ap(o), ap(s), F_.Identity, scale=f)
+    ts(ap("BOw"), ap("BO"), col("wc", 0), A_.mult, 0.5, A_.mult)
+    ts(ap("In16"), ap("I"), -1.0, A_.mult)
+    if not cfg["MV"]:
+        ts(ap("Ih16"), ap("I"), 0.5, A_.mult)
+    V("memset", ap("jk", 0, 16), -EVEN)
+    cp(ap("cn"), ap("jk", 0, 16))
+    ts(ap("jk", 0, 128), x128, pc, A_.is_ge)
+    tt(ap("Tri"), ap("jk", 0, 128), ap("BO"), A_.mult)
+    ts(ap("jk", 128, 256), x128, pc, A_.subtract, 1.0, A_.is_equal)
+    ts(ap("Sh"), ap("jk", 128, 256), col("cf", 6), A_.mult, -BIG, A_.mult)
+    ts(ap("W15"), x128, -1.0, A_.is_ge, col("cf", 5), A_.mult)
+    ts(ap("E8"), ap("X16"), col("cf", 9), A_.is_equal)
+    cp(ap("thf", 0, 2, 1, (0, 8)), ap("thi", 0, 2, 1, (0, 8)))
+    mm([(ap("p2", 0, 2), ap("E8", 0, 128, 1, (0, 8)), ap("thf", 0, 2, 1, (0, 8)))])
+    ts(col("bs", 2), ap("p2", 0, 1), -1.0, A_.mult, -0.5, A_.add)
+    ts(col("bs", 1), ap("p2", 1, 2), -1.0, A_.mult, col("cf", 10), A_.add)
+    ts(col("bs", 0), col("bs", 2), col("cf", 6), A_.mult, col("cf", 5), A_.add)
+    iota(ap("ai", 0, 16), [[16, 16]], 0, 0)
+    ts(ap("ai", 16, 32), ap("ai", 0, 16), kc, A_.add)
+    ts(ap("bL"), ap("ai", 16, 32), 16.0, A_.mult)
+    ts(ap("bI", 16, 32), ap("ai", 16, 32), 8.0, A_.mult)
+    for c in range(len(CH)):
+        ts(ap("bI", J[c] // 16, J[c + 1] // 16), ap("ai", 16 + J[c] // 16, 16 + J[c + 1] // 16), 2.0, A_.mult,
+           -2.0 * J[c], A_.add)
+    V("memset", ap("km"), 1.0)
+    V("memset", ap("km", 0, 1024, 16), 0.0)
+    XO = [16 * J[c] + PAD * (c + 1) for c in range(len(CH))]
+    for c in range(len(CH)):
+        V("memset", ap("xb", XO[c] - PAD, XO[c]), 0.0)
+        if cfg["P2"][c]:
+            V("memset", ap("dl", XO[c] + 16 * CH[c], XO[c] + 16 * CH[c] + PAD), 0.0)
+    if any(cfg["P2"]):
+        act(ap("I4n"), ap("I"), F_.Identity, scale=-4096.0)
+        V("memset", ap("Zr"), 0.0)
+        ts(ap("Wl"), ap("W"), col("cf", 5), A_.mult, -4096.0, A_.mult)
+        ts(col("bs", 3), col("bs", 1), -4096.0, A_.add)
+    V("memset", ap("nd"), 0)
+    cp(ap("E"), ap("Ei"))
+    iota(ap("Lr"), [[0, 16], [1, 16]], 0, 0)
+    ts(ap("Cm"), ap("Lr"), kc, A_.is_ge, 4096.0, A_.mult)
+    iota(ap("Tv"), [[1, 2048]], 0, 0)
+    ops[-1]["aft"] = [i for i, o in enumerate(ops[:-1]) if o["eng"] == "G"]
+
+    Xw = ap("X")
+    for t in range(STEPS):
+        last = t == STEPS - 1
+        o16, o32 = 16 * (t % 2), 32 * (t % 2)
+        Gf = ap("Gf", 512 * t - 512, 512 * t) if t else ap("G0")
+        NG = cfg["NG"] if t else [0, len(CH)]
+        cLo = {}
+        where[0], where[1] = "n", "a"
+        if last:
+            dma(ap("X2"), Xw, 524288)
+        for gi in range(len(NG) - 1):
+            j0, j1 = J[NG[gi]], J[NG[gi + 1]]
+            a0, a1 = j0 // 16, j1 // 16
+            na = a1 - a0
+
+            def L(name, o=0):
+                return ap(name, o + a0, o + a1)
+            if t == 0:
+                mm([(ap("p7", 0, na), sel("Ww", l), ap("q", j0 + l, j1, 16)) for l in range(16)])
+            else:
+                mm([(ap("p7", 0, na), ap("BOw"), ap("cn", 0, na))] +
+                   [(ap("p7", 0, na), sel("Wh", l), ap("q2", j0 + l, j1, 16)) for l in range(16)])
+            cp(L("u0"), ap("p7", 0, na))
+            ts(L("u"), L("u0"), 2047, A_.bitwise_and)
+            ts(L("t1"), L("u"), 1184.0, A_.add)
+            tt(L("t2"), L("t1"), L("u"), A_.mult)
+            src = "t2"
+            if t > 0:
+                ts(L("t3"), L("t2"), col("Ac", 0), A_.add)
+                src = "t3"
+            ts(L("nI"), L(src), 5, A_.arith_shift_right, 2047, A_.bitwise_and)
+            cp(L("n16", o16), L("nI"))
+            if not last:
+                cp(L("nh", o16), L("nI"))
+            cp(ap("Dg", j0, j1), ind(ap("Dw", 0, 2048), L("n16", o16)))
+            mm([(ap("p7", 0, na), sel("WD0", l), ap("Dg", j0 + l, j1, 16)) for l in range(16)])
+            if t == 0:
+                cp(ap("cL", 0, 16), ap("p7", 0, 16))
+                dma(ap("Dw", 0, 2048, 1, (1, 128, 16)), ap("Dl", 0, 128), 65536)
+                cp(ap("Dg2"), ind(ap("Dw", 0, 2048), L("n16", o16)))
+                mm([(ap("p4", 0, 16), sel("WD1", l), ap("Dg2", l, 256, 16)) for l in range(16)])
+                cp(ap("cL", 16, 32), ap("p4", 0, 16))
+            elif gi == 0 and cfg["oc"]:
+                cp(ap("cL", 2 * a0, 2 * a0 + na), ap("p7", 0, na))
+                mm([(ap("p7", na, 2 * na), sel("WD1", l), ap("Dg", j0 + l, j1, 16)) for l in range(16)])
+                cp(ap("cL", 2 * a0 + na, 2 * a1), ap("p7", na, 2 * na))
+            else:
+                mm([(ap("p7", na, 2 * na), sel("WD1", l), ap("Dg", j0 + l, j1, 16)) for l in range(16)])
+                cp(ap("cL", 2 * a0, 2 * a1), ap("p7", 0, 2 * na))
+            for c in range(NG[gi], NG[gi + 1]):
+                cLo[c] = (a0 + J[c] // 16, a0 + J[c] // 16 + na)
+            ts(L("ub"), L("u0"), 1, A_.bitwise_and)
+            ts(L("ub", 16), L("u0"), 7, A_.bitwise_and)
+        tt(ap("uc"), ap("ub"), ap("bI"), A_.add)
+        cp(ap("cx16", o32, o32 + 32), ap("uc"))
+        for gi in range(len(cfg["PG"]) - 1):
+            c = cfg["PG"][gi]
+            j0, j1 = J[c], J[cfg["PG"][gi + 1]]
+            na = (j1 - j0) // 16
+            cp(ap("P16", j0, j1), ind(ap("G"), ap("cL", cLo[c][0], cLo[c][0] + na)))
+            cp(ap("B16", j0, j1), ind(Gf, ap("cL", cLo[c][1], cLo[c][1] + na)))
+            cp(ap("Pf", j0, j1), ap("P16", j0, j1))
+            cp(ap("Bf", j0, j1), ap("B16", j0, j1))
+        where[1] = "d"
+        if not last:
+            either(ap("nr"), ind(ap("Tv"), ap("n16", o16, o16 + 16)))
+            for c in range(len(CH)):
+                either(ap("Vc", J[c], J[c + 1]), ind(ap("Tv", 2 * J[c], 2 * J[c + 1]), ap("cx16", o32 + J[c] // 16, o32 + J[c + 1] // 16)))
+            mm([(ap("p7", 0, 256), ap("I"), ap("Cm"))] +
+               [(ap("p7", l, 256, 16), ap("I16"), ap("nh", o16, o16 + 16)) for l in range(16)])
+            tt(ap("eq"), ap("nr"), ap("p7", 0, 256), A_.is_equal)
+            mm([(ap("p7", 0, 16), ap("I16"), ap("nh", o16, o16 + 16))] +
+               [(ap("p7", 0, 16), ap("I4"), ap("eq", l, 256, 16)) for l in range(15)])
+            ts(ap("nd", 0, 32, 2), ap("p7", 0, 16), col("cf", 8), A_.min)
+            for a in range(15, -1, -1):
+                cp(ind(ap("Dw"), ap("nd", 2 * a, 2 * a + 1)), ap("Vc", 16 * a, 16 * a + 16))
+            dma(ap("Ds"), ap("Dw", 0, 2048, 1, (0, 128, 16)), 65536)
+            send(ap("Dl", 128 * t + 128, 128 * t + 256), ap("Ds"), t + 2)
+            dma(ap("Dw", 0, 2048, 1, (1, 128, 16)), ap("Dl", 128 * t + 128, 128 * t + 256), 65536)
+        SUB = cfg["SUB"]
+        for c in range(len(CH)):
+            j0, j1, nc = J[c], J[c + 1], CH[c]
+            a0, a1, na = j0 // 16, j1 // 16, CH[c] // 16
+            b0, b1, xo = 16 * j0, 16 * j1, XO[c] - 16 * j0
+            where[0], where[1] = "c%d" % c, "a"
+
+            def Kc(name):
+                return ap(name, j0, j1)
+            subs = [(s, min(s + SUB, j1)) for s in range(j0, j1, SUB)]
+            for si, (s0, s1) in enumerate(subs):
+                xs_ = ap("xb", xo + 16 * s0, xo + 16 * s1)
+                either(xs_, ind(Xw, ap("P16", s0, s1)))
+                dl_ = ap("dl", xo + 16 * s0, xo + 16 * s1)
+                if cfg["YS"][c]:
+                    either(dl_, ind(Xw, ap("B16", s0, s1)))
+                    o = ap("p%d" % (5 + si % 2), 0, 16 * (s1 - s0))
+                    mm([(o, ap("In"), xs_), (o, ap("I"), dl_)])
+                    act(ap("rl", 16 * s0, 16 * s1), o, F_.Abs)
+                    continue
+                tt(dl_, ind(Xw, ap("B16", s0, s1)), xs_, A_.subtract)
+                if cfg["ABS"][c]:
+                    act(ap("rl", 16 * s0, 16 * s1), dl_, F_.Abs)
+                else:
+                    either(ap("rl", 16 * s0, 16 * s1), dl_, True)
+            for s0 in range(b0, b1, cfg["SC"]):
+                s1 = min(s0 + cfg["SC"], b1)
+                V("tensor_tensor_scan", ap("pm", s0, s1), ap("xb", xo + s0 - 1, xo + s1 - 1), ap("km", 0, s1 - s0), 0.0, A_.max, A_.mult)
+        for c in range(len(CH)):
+            j0, j1, nc = J[c], J[c + 1], CH[c]
+            a0, a1, na = j0 // 16, j1 // 16, CH[c] // 16
+            b0, b1, xo = 16 * j0, 16 * j1, XO[c] - 16 * j0
+            where[0], where[1] = "c%d" % c, "a"
+
+            def Kc(name):
+                return ap(name, j0, j1)
+            subs = [(s, min(s + SUB, j1)) for s in range(j0, j1, SUB)]
+            late = cfg["EP"] and c == len(CH) - 1 and not last
+            gf = ap("Gf", 512 * t + 2 * j0, 512 * t + 2 * j1)
+            if late:
+                send(gf, ap("G", 2 * j0, 2 * j1), t + 2)
+                send(ap("clf", 16 * t + a0, 16 * t + a1), ap("cx16", o32 + a0, o32 + a1), t + 2)
+            p0 = ap("p0", 0, nc)
+            if cfg["ABS"][c] or cfg["YS"][c]:
+                mm([(p0, sel("W", k), ap("rl", b0 + k, b1, 16)) for k in range(15)])
+            else:
+                mm([(p0, sel("Wn", k), ap("dl", xo + b0 + k, xo + b1, 16)) for k in range(15)], True, False)
+                mm([(p0, sel("W2", k), ap("rl", b0 + k, b1, 16)) for k in range(15)], False, True)
+            where[1] = "b"
+            pb = "p0" if cfg["ZP"] == 2 else "p1"
+            act(Kc("sg"), p0, F_.Sign, bias=col("bs", 0))
+            mm([(ap(pb, 0, nc), ap("Tri"), Kc("sg"))])
+            act(Kc("lts"), ap(pb, 0, nc), F_.Relu, bias=col("cf", 7), scale=-1.0)
+            mm([(ap(pb, 0, na), ap("I"), ap("bL", 0, na))] +
+               [(ap(pb, 0, na), sel("W", l), ap("lts", j0 + l, j1, 16)) for l in range(16)])
+            sL = ap("sL", a0, a1)
+            cp(sL, ap(pb, 0, na))
+            tt(Kc("mq"), ind(ap("pm", b0, b1), sL), Kc("q"), A_.subtract)
+            either(Kc("xs"), ind(ap("xb", xo + b0, xo + b1), sL))
+            act(Kc("d"), Kc("mq"), F_.Abs)
+            p2 = ap("p2", 0, nc)
+            if cfg["LS"]:
+                either(Kc("ds"), ind(ap("dl", xo + b0, xo + b1), sL))
+                pn = ap("p2", nc, 2 * nc)
+                mm([(p2, ap("I"), Kc("xs")), (p2, ap("In"), Kc("d")), None,
+                    (pn, ap("I"), Kc("ds")), (pn, ap("In"), Kc("d"))] + ([] if cfg["YS"][c] else [(pn, ap("I"), Kc("xs"))]))
+                act(ap("al", 2 * j0, 2 * j1), ap("p2", 0, 2 * nc), F_.Abs)
+                mm([(pn, ap("I16"), Kc("Bf")), (pn, ap("In16"), Kc("Pf")), None, (p2, ap("IB"), Kc("lts")),
+                    (p2, ap("BO"), ap("al", 2 * j0, 2 * j0 + nc)), (p2, ap("BOn"), ap("al", 2 * j0 + nc, 2 * j1))])
+            else:
+                pn = ap("p2", nc, 2 * nc)
+                if cfg["YS"][c]:
+                    either(Kc("ys"), ind(ap("dl", xo + b0, xo + b1), sL))
+                else:
+                    tt(Kc("ys"), ind(ap("dl", xo + b0, xo + b1), sL), Kc("xs"), A_.add)
+                tt(Kc("mx"), Kc("xs"), Kc("d"), A_.max)
+                tt(Kc("my"), Kc("ys"), Kc("d"), A_.max)
+                mm([(pn, ap("I16"), Kc("Bf")), (pn, ap("In16"), Kc("Pf")), None,
+                    (p2, ap("IB"), Kc("lts")), (p2, ap("BOn"), Kc("xs")), (p2, ap("BO"), Kc("ys"))], True, False)
+                mm([(p2, ap("BO2"), Kc("mx")), (p2, ap("BOn2"), Kc("my"))], False, True)
+            act(Kc("dm"), Kc("d"), F_.Identity, bias=EVEN - 0.5)
+            if cfg["MV"]:
+                ts(Kc("m01"), p2, 0.0, A_.is_gt)
+            elif last:
+                act(Kc("m01"), p2, F_.Sign, bias=-0.5)
+            else:
+                act(Kc("m01"), p2, F_.Sign, bias=-0.5, accum_out=col("ac", c))
+            tt(Kc("tz"), pn, Kc("m01"), A_.mult)
+            df = Kc("df")
+
+            def names(o):
+                if cfg["MV"]:
+                    return [(o, ap("I16"), Kc("Pf")), (o, ap("I16"), Kc("tz"))]
+                return [(o, ap("Ih16"), Kc("Pf")), (o, ap("Ih16"), Kc("Bf")), (o, ap("Ih16"), Kc("tz"))]
+            both = cfg["P2"][c] and not cfg["YS"][c]
+            if not both or cfg["ZP"] != 2:
+                mm(names(p2))
+            if not both:
+                cp(Kc("Z16"), p2)
+            if cfg["ZP"] == 2:
+                df = ap("p1", 0, nc)
+                mm([(df, ap("In16"), Kc("E"))] + names(df))
+            else:
+                tt(df, p2, Kc("E"), A_.subtract)
+            if not last and c == len(CH) - 1:
+                if cfg["MV"]:
+                    act(ap("jk"), ap("m01"), F_.Copy, accum_out=col("ac", 0))
+                    mm([(ap("p2", 0, 1), ap("W15"), col("ac", 0))])
+                    act(col("Ac", 0), ap("p2", 0, 1), F_.Identity, scale=32.0)
+                else:
+                    mm([(ap("p2", 0, 1), ap("W15"), col("ac", e)) for e in range(len(CH))])
+                    act(col("Ac", 0), ap("p2", 0, 1), F_.Identity, scale=16.0, bias=32768.0)
+            where[1] = "c"
+            p3 = ap("p3", 0, nc)
+            per = 512 // nc
+            ks = [list(range(k, min(k + per, 16))) for k in range(1, 16, per)]
+            if both:
+                py = ap("p3", nc, 2 * nc)
+                mm([(ap("p3", 0, 2 * nc), ap("Zr"), ap("km", 0, 2 * nc)), (p3, ap("Sh"), Kc("lts")), (py, ap("Sh"), Kc("lts"))], True, False)
+                for bi, kk in enumerate(ks):
+                    bank = "p%d" % (5 + c % 2)
+                    k0, k1 = b0 + kk[0] * nc, b0 + (kk[-1] + 1) * nc
+                    outs = [(ap(bank, i * nc, i * nc + nc), k) for i, k in enumerate(kk)]
+                    xd, yd = [], []
+                    for (o, k) in outs:
+                        one = [None, (o, ap("I"), ap("xb", xo + b0 + k, xo + b1, 16)), (o, ap("In"), Kc("d"))]
+                        xd += one
+                        yd += one + [(o, ap("I"), ap("dl", xo + b0 + k, xo + b1, 16))]
+                    mm(xd[1:])
+                    act(ap("az", k0, k1), ap(bank, 0, len(kk) * nc), F_.Abs)
+                    bank = "p%d" % (5 + (c + 1) % 2)
+                    mm([e and (ap(bank, e[0][2], e[0][3]), e[1], e[2]) for e in yd[1:]])
+                    act(ap("zb", k0, k1), ap(bank, 0, len(kk) * nc), F_.Abs)
+                    mm([(p3, sel("W", k), ap("az", b0 + k * nc, b0 + k * nc + nc)) for k in kk], False, False)
+                    mm([(py, sel("W", k), ap("zb", b0 + k * nc, b0 + k * nc + nc)) for k in kk], False, False)
+                mm([(p3, ap("I4n"), Kc("m01")), (py, ap("I4"), Kc("m01"))], False, True)
+                act(ap("sg2", 2 * j0, 2 * j1), ap("p3", 0, 2 * nc), F_.Sign, bias=col("bs", 3))
+                mm([(ap("p4", 0, nc), ap("Tri"), ap("sg2", 2 * j0, 2 * j0 + nc)), (ap("p4", 0, nc), ap("Tri"), ap("sg2", 2 * j0 + nc, 2 * j1))])
+                act(Kc("lte"), ap("p4", 0, nc), F_.Relu, bias=col("cf", 7), scale=-0.5)
+            else:
+                for si, (s0, s1) in enumerate(subs):
+                    zs = ap("zb", 16 * s0, 16 * s1)
+                    either(zs, ind(Xw, ap("Z16", s0, s1)))
+                mm([(p3, ap("Sh"), Kc("lts"))], True, False)
+                for bi, kk in enumerate(ks):
+                    bank = "p%d" % (5 + (bi + c) % 2)
+                    grp = []
+                    for i, k in enumerate(kk):
+                        o = ap(bank, i * nc, i * nc + nc)
+                        grp += [None, (o, ap("I"), ap("zb", b0 + k, b1, 16)), (o, ap("In"), Kc("d"))]
+                    mm(grp[1:])
+                    if bi % 2 == 1 and bi // 2 < cfg["AV"][c]:
+                        mm([e for k in kk for e in ((p3, sel("Wn", k), ap("zb", b0 + k, b1, 16)), (p3, sel("W", k), Kc("d")))], False, False)
+                        ts(ap("az", b0 + kk[0] * nc, b0 + (kk[-1] + 1) * nc), ap(bank, 0, len(kk) * nc), 0.0, A_.max)
+                        mm([(p3, sel("W2", k), ap("az", b0 + k * nc, b0 + k * nc + nc)) for k in kk], False, bi == len(ks) - 1)
+                        continue
+                    act(ap("az", b0 + kk[0] * nc, b0 + (kk[-1] + 1) * nc), ap(bank, 0, len(kk) * nc), F_.Abs)
+                    mm([(p3, sel("W", k), ap("az", b0 + k * nc, b0 + k * nc + nc)) for k in kk], False, bi == len(ks) - 1)
+                act(ap("sg2", 2 * j0, 2 * j0 + nc), p3, F_.Sign, bias=col("bs", 1))
+                mm([(ap("p4", 0, nc), ap("Tri"), ap("sg2", 2 * j0, 2 * j0 + nc))])
+                act(Kc("lte"), ap("p4", 0, nc), F_.Relu, bias=col("cf", 7), scale=-1.0)
+            where[1] = "d"
+            tt(Kc("te"), df, Kc("lte"), A_.mult)
+            tt(Kc("E"), Kc("E"), Kc("te"), A_.add)
+            if late:
+                ef = ap("Ef", 128 * t, 128 * t + nc)
+                send(ef, Kc("E"), t + 2)
+            cp(ind(ap("G", 2 * j0, 2 * j1), ap("cx16", o32 + a0, o32 + a1)), Kc("E"))
+            if late:
+                cp(ind(gf, ap("clf", 16 * t + a0, 16 * t + a1)), ef)
+            elif not last:
+                send(gf, ap("G", 2 * j0, 2 * j1), t + 2)
+            else:
+                dma(ap("yl", 2 * j0, 2 * j1), ap("G", 2 * j0, 2 * j1), 1024 * nc)
+            mm([(ap("p4", 0, na), ap("I"), ap("bL", 0, na))] +
+               [(ap("p4", 0, na), sel("W", l), ap("lte", j0 + l, j1, 16)) for l in range(16)])
+            if both:
+                pe = ap("p4", 16, 16 + na)
+                mm([(pe, ap("I"), ap("bL", 0, na))] + [(pe, sel("Wl", l), ap("m01", j0 + l, j1, 16)) for l in range(16)] +
+                   [(pe, sel("W", l), ap("lte", j0 + l, j1, 16)) for l in range(16)])
+            eL = ap("eL", a0, a1)
+            ts(eL, ap("p4", 0, na), -1.0, A_.add)
+            if both:
+                eD = ap("eD", a0, a1)
+                ts(eD, ap("p4", 16, 16 + na), 4095.0, A_.add, 16.0 * nc, A_.min)
+                tt(Kc("vq"), ind(ap("xb", xo + b0, xo + b1), eL), Kc("dm"), A_.add)
+                tt(Kc("q2"), ind(ap("dl", xo + b0, xo + b1 + PAD), eD), Kc("vq"), A_.add)
+            else:
+                tt(Kc("q2"), ind(ap("zb", b0, b1), eL), Kc("dm"), A_.add)
+            if last:
+                ts(Kc("q"), Kc("q2"), 0.5, A_.mult, -EVEN / 2, A_.add)
+                dma(ap("yq", j0, j1), Kc("q"), 256 * nc)
+        where[0], where[1] = "x", "a"
+        if not last:
+            ts(ap("q"), ap("q2"), 0.5, A_.mult, -EVEN / 2, A_.add)
+        cxl = ap("cx16", o32 + 16, o32 + 32)
+        tt(ap("xo"), ind(Xw, cxl), ap("dm"), A_.add)
+        ts(ap("x2"), ap("xo"), 0.5, A_.mult, -EVEN / 2, A_.add)
+        cp(ind(ap("X2") if last else Xw, cxl), ap("x2"))
+    dma(ap("yx", 0, 1024), ap("X2", 0, 1024), 262144)
+    dma(ap("yx", 1024, 2048), ap("X2", 1024, 2048), 262144)
+    return ops
+
+
+def depend(ops):
+    n = len(ops)
+    pred = [set() for _ in range(n)]
+    hist = {}
+    for i, o in enumerate(ops):
+        if o["kind"] == "arr":
+            pred[i].add(o["x"])
+        for (name, lo, hi) in o["rd"]:
+            for (j, l2, h2, w) in hist.get(name, []):
+                if w and l2 < hi and lo < h2:
+                    pred[i].add(j)
+        for (name, lo, hi) in o["wr"]:
+            keep = []
+            for e in hist.get(name, []):
+                if e[1] < hi and lo < e[2]:
+                    pred[i].add(e[0])
+                    if lo <= e[1] and e[2] <= hi:
+                        continue
+                keep.append(e)
+            hist[name] = keep
+        for (name, lo, hi) in o["rd"]:
+            hist.setdefault(name, []).append((i, lo, hi, False))
+        for (name, lo, hi) in o["wr"]:
+            hist.setdefault(name, []).append((i, lo, hi, True))
+        pred[i].discard(i)
+    return pred
+
+
+def variant(o, e):
+    return o if o["eng"] == e else o["alt"]
+
+
+def prepare(ops, pred, K):
+    n = len(ops)
+    succ = [[] for _ in range(n)]
+    left = [0] * n
+    for i in range(n):
+        for j in sorted(set(pred[i]) | set(ops[i].get("aft", []))):
+            kind = 0 if ops[i]["kind"] == "arr" else 1 if (ops[j]["eng"] == "P" and ops[i]["eng"] == "P") or j not in pred[i] else 2
+            succ[j].append((i, kind))
+            left[i] += 1
+    prio = [0.0] * n
+    for i in range(n - 1, -1, -1):
+        gap = (0.0, ops[i]["occ"], ops[i]["lat"] + K["wake"])
+        prio[i] = max([gap[k] + prio[s] for (s, k) in succ[i]] + [ops[i]["lat"]])
+    return succ, left, prio
+
+
+def schedule(ops, prep, K, bias):
+    n = len(ops)
+    succ, left = prep[0], list(prep[1])
+    prio = [prep[2][i] + bias.get(ops[i].get("key"), 0) + bias.get(ops[i].get("grp"), 0) for i in range(n)]
+    other = [prio[i] + bias.get("alt", -2000) + bias.get("~" + ops[i]["key"], 0) if "alt" in ops[i] else 0.0 for i in range(n)]
+    ready = [0.0] * n
+    start = [0.0] * n
+    free = {e: 0.0 for e in "VSPGY"}
+    order = {e: [] for e in "VSPGY"}
+    pool = {e: [] for e in "VSPGY"}
+    end = [0.0]
+
+    def release(i, o):
+        gap = (0.0, o["occ"], o["lat"] + K["wake"])
+        end[0] = max(end[0], start[i] + o["lat"])
+        for (s, k) in succ[i]:
+            if start[i] + gap[k] > ready[s]:
+                ready[s] = start[i] + gap[k]
+            left[s] -= 1
+            if left[s] == 0:
+                if ops[s]["eng"] is None:
+                    start[s] = ready[s]
+                    release(s, ops[s])
+                else:
+                    pool[ops[s]["eng"]].append(s)
+                    if "alt" in ops[s]:
+                        pool["V"].append(s)
+    for i in range(n):
+        if left[i] == 0:
+            pool[ops[i]["eng"]].append(i)
+    look = bias.get("look", 40)
+    while True:
+        best = None
+        for e in "SVPGY":
+            if pool[e]:
+                tm = max(free[e], min([ready[i] for i in pool[e]]))
+                if best is None or tm < best[0]:
+                    best = (tm, e)
+        if best is None:
+            break
+        tm, e = best
+        i, top = -1, None
+        for c in pool[e]:
+            if ready[c] <= tm + look:
+                p = prio[c] if ops[c]["eng"] == e else other[c]
+                if top is None or p > top:
+                    i, top = c, p
+        pool[e].remove(i)
+        if "alt" in ops[i]:
+            pool["S" if e == "V" else "V"].remove(i)
+        o = variant(ops[i], e)
+        start[i] = max(tm, ready[i])
+        free[e] = start[i] + o["occ"]
+        order[e].append(i)
+        release(i, o)
+    return order, start, end[0]
+
+
+PLAN = []
+
+
+def rank_program(g, core, T, topo):
+    rank = T.rank_of(core)
+    if rank is None:
+        return
+    if not PLAN:
+        ops = build(CFG, COST)
+        pred = depend(ops)
+        PLAN.append((ops, pred, schedule(ops, prepare(ops, pred, COST), COST, BIAS)[0]))
+    ops, pred, order = PLAN[0]
+    queue = {"V": g.vector, "S": g.scalar, "P": g.tensor, "G": g, "Y": g.sync}
+
+    def engines(src, dst):
+        return len(topo.engines(T.cores[src % N], T.cores[dst % N]))
+    done, nm, na = {}, 0, 0
+    for e in order:
+        k = 0
+        for i in order[e]:
+            o = ops[i]
+            if o["kind"] == "c":
+                k += 1
+                done[i] = (e, k)
+            elif o["kind"] == "dma":
+                done[i] = ("m%d" % nm, 16)
+                nm += 1
+            else:
+                done[i] = ("m%d" % nm, engines(rank, rank - o["x"][1]))
+                done[i + 1] = ("a%d" % na, engines(rank + o["x"][1], rank))
+                nm += 1
+                na += 1
+    seen_all = {}
+    for e in order:
+        qu, seen = queue[e], {}
+        for i in order[e]:
+            o = ops[i]
+            need = {}
+            for j in pred[i]:
+                if e == "P" and ops[j]["eng"] == "P":
+                    continue
+                s, v = done[j]
+                need[s] = max(need.get(s, 0), v)
+            for s in sorted(need):
+                if seen.get(s, 0) < need[s]:
+                    qu.wait_ge(T.sem[s], need[s])
+                    seen[s] = need[s]
+                    seen_all[s] = max(seen_all.get(s, 0), need[s])
+            s, v = done[i]
+            if o["kind"] == "send":
+                dst = T.cores[(rank - o["x"][1]) % N]
+                rid, pid = topo.addr(dst, core)
+                g.remote_dma(real(T, o["x"][0]), real(T, o["calls"][0][1][1]), T.sem[done[i + 1][0]], T.sem[s], pid, rid,
+                             topo.mask(core, dst))
+                continue
+            for (m, args, kw) in variant(o, e)["calls"]:
+                a = [real(T, x) if is_ap(x) else x for x in args]
+                w = {key: (real(T, x) if is_ap(x) else x) for key, x in kw.items()}
+                if m == "matmul":
+                    ins = qu.matmul(*a)
+                elif m == "activation":
+                    ins = qu.activation(*a, **w)
+                elif m == "iota":
+                    ins = qu.iota(*a, **w)
+                elif m == "dma_start":
+                    ins = qu.dma_start(*a)
+                elif m == "memset":
+                    ins = qu.memset(*a)
+                elif m == "tensor_copy":
+                    ins = qu.tensor_copy(*a)
+                elif m == "tensor_tensor":
+                    ins = qu.tensor_tensor(*a)
+                elif m == "tensor_scalar":
+                    ins = qu.tensor_scalar(*a)
+                else:
+                    ins = qu.tensor_tensor_scan(*a)
+            ins.then_inc(T.sem[s], 16 if o["kind"] == "dma" else 1)
+    total = {}
+    for (s, v) in done.values():
+        total[s] = max(total.get(s, 0), v)
+    for s in sorted(total):
+        if seen_all.get(s, 0) < total[s] or s in order:
+            g.sync.wait_ge(T.sem[s], total[s])

@@ -3,83 +3,70 @@ from concourse.bass import DstId, RemoteDMATransfer
 from concourse.mybir import dt, AluOpType, AxisListType, ActivationFunctionType
 
 N, STEPS, C = 8, 4, 256
-F16 = "float16"
+F16, BF, F32, I32, U16 = "float16", "bfloat16", "float32", "int32", "uint16"
 CFG = {
-    "CH": [64, 64, 64, 64],
-    "NG": [0, 3, 4],
-    "SUB": 32,
-    "ABS": [1, 0, 0, 0],
-    "PG": [0, 1, 3, 4],
-    "LS": 1,
-    "ZP": 1,
-    "SC": 1024,
-    "oc": 1,
-    "P2": [0, 0, 0, 1],
-    "AV": [0, 0, 1, 1],
-    "YS": [0, 1, 0, 0],
-    "EP": 1,
-    "MV": 0,
+    "CH": [128, 128],
+    "NG": [0, 1, 2],
+    "SX": [[32, 48, 48], [48, 48, 32]],
+    "SZ": [[64, 64], [32, 32, 32, 32]],
+    "U1": [64, 64],
+    "U2": [64, 64],
+    "SC": [64, 64],
+    "AB": [1, 1],
+    "LS": [0, 0],
+    "ET": [1, 1],
+    "CC": [1, 1],
+    "EP": [0, 1],
+    "SR": 128,
+    "D3": 1,
+    "AV": [0, 0],
+    "PS": [0, 0],
+    "MP": [0, 0],
+    "D2": [0, 0],
+    "ONV": ["WD0_0", "zb3584", "zb2560", "q0", "q128", "x2_0"],
+    "DG": 520,
 }
-CFG.update({'CH': [96, 96, 64], 'NG': [0, 1, 3], 'SUB': 32, 'ABS': [1, 1, 0], 'PG': [0, 1, 3], 'LS': 0, 'ZP': 2, 'SC': 1024, 'oc': 1,
-            'P2': [0, 0, 0], 'AV': [0, 0, 0], 'YS': [0, 0, 0], 'EP': 0, 'MV': 0})
-BIAS = {'~SVc192n': -4000, 'Sd96c1': -1000, 'VbI0i': -4000, 'Sdm192c2': 3500, 'c2c': -1000, 'Vmq192c2': -4000, 'Vt10n': 4000, 'Pp00c1': 1000, 'GGf0c0': 4000, 'Szb3072c2': -4000, 'VDg20n': 1000, 'Pp10c2': -2000, 'VDw0n': -2000, 'Vpm2560c1': 500, 'VG0i': -1000, '~Srl3584c2': -2000, 'Vuc0n': -4000, '~Sxb3120c2': 1500, 'Slts96c1': -1000, 'c2d': 4500, 'Sxb2080c1': -500, 'c0a': 1000, 'Vu00n': 1000, 'Szb0c0': -4000, 'Saz2592c1': -1000, 'VeL12c2': -4000, '~Szb1024c0': 1000, 'Ssg20c0': -2000, 'Vnh6n': -2000, '~Sxs192c2': -4000, '~Szb1536c1': 4000, 'Sd0c0': 4000, 'Vnh16n': -2000, 'nd': 1000, 'VG192c1': -500, 'Vx20x': 500, 'Vpm1024c0': 500, 'VE0i': 500, 'Sd192c2': 500, 'SIn0i': -1000, 'Vpm3072c2': -4000, 'Vdl2080c1': 2000, 'Vcf4i': 1000, 'VWh0i': -1000, 'Sm010c0': 4000, 'Pp50c0': 500, 'Vkm0i': -500, 'Srl3584c2': 1000, 'Pp40n': 500, 'c0d': -1000, 'SVc96n': 4000}
+BIAS = {}
+PERIOD = 2900
+TIMES = """
+ci0i@-8003 Xr0i@-7922 Dw0i@-7751 Dw1560i@-7549 wc0id@-7094 ci2i@-7023 ai0i*@-6781 ci1i@-6568 pm2064i@-6548 Dw1040i@-6508 cf0i@-6467 W0i@-6397 cf8i*@-5750 bI16i@-5689 I0i@-5507 nd0i@-5477 Dw520i@-5467 Ww0i@-5265 pm0i@-5245 K16_0i@-5204 jk128i@-5053 Ds0id@-4790 Gi0id@-4618 X16_0i@-4396 Dlis@-4386 Gi256id@-4305 Gais@-4214 Gais.1@-4164 Lr0i@-3618 q0id@-3517 Tv0i@-3052 bL0i@-2830 cf11i@-2769 Tv1024i@-2557 In16_0i@-2274 WD0_0i@-2213 bI0i@-2143 I4_0i*@-1769 W15_0i@-1668 Tc0i@-1526 cf10i*@-1516 jk0i@-1355 Tc1024i@-960 I16_0i@-627 Dw0id@-516 u0_0n@-506 X0_0id@-496 pu0n@-475 u0n@-455 ub0n@-445 cf7i*@-425 Wh0i@-405 t3_0n@-395 Ei0id@-384 t2_0n@-354 t1_0n@-324 bI8i@-314 ub16n@-304 cL0n@-294 thi0id@-273 nI0n@-263 Dg0n@-243 q0b0@-233 Ih16_0i*@-213 n16_0n@-203 Dg128n*@-182 q128b1@-172 WD1_0i@-142 BO0i@-132 u8n@-122 G0i@-112 t1_8n@-102 cf9i@-91 u0_8n@-81 PB0n@-51 Dw0nd@-41 pc0n@-31 pu1n@-21 t2_8n@-11 Sh0i@0 cf17i@10 uc0n@20 t3_8n@30 T8_0i@40 BOn2_0i@60 E8_0i@80 nI8n@90 cxn@101 xb0a0@121 Dg2_128n*@141 thf0i@161 BOn0i*@171 po0n@202 pc1n@212 p3_0i@222 km0i@232 Dg2_0n@242 n16_8n@252 T8n0i*@272 Cm0i@282 xb512a0@303 dl512a0@353 po1n@363 cL16n@373 km15i@383 nr0d@394 xb1280a0@404 bs0i@414 nh0d@424 cL8n@434 PB256n@444 p4_0d@454 bs2i*@464 BO2_0i*@474 xb2816a1@485 xb2048a1@495 PB128n@505 dl0a0@515 rl512a0@525 p4_0d.1@545 eq0d@565 rl0a0@575 cL24n@586 dl1280a0@606 rl1280a0@616 nd0d@636 PB384n@646 pm1a0@656 Vc0d@666 p0_0b0@677 dl2816a1@707 p0_64b0@717 p0_0b0.1@727 dl2048a1@737 Dw0d@767 xb3584a1@788 bs1i*@798 m01_0b0@808 dl3584a1@818 Dx1024i@828 sg0b0@838 Dw0d.1@848 sL0b0@858 pm1025a0@868 rl2816a1@879 Dw0d.2@889 PBf0n@899 lts0b0@909 rl2048a1@919 rl3584a1@939 Dw0d.3@959 p0_0b0.2@970 bs3i@980 Dw0d.4@990 mq0b0@1000 pm2065a1@1030 ab0b0@1040 ab128b0@1050 rb128b0@1060 rb0b0@1071 Dw0d.5@1081 Dw0d.11@1091 d0b0@1101 Dw0d.6@1111 lts128b1@1121 dm0b0@1141 p1_64b1@1162 p1_0b1@1172 Dw0d.15@1192 pm3089a1@1202 p1_0b1.1@1212 sg128b1@1222 p0_0b0.3@1242 In0i@1252 p0_128b0@1263 p1_0b1.2@1273 zb2048c1*@1283 Dw0d.7@1293 ab256b1@1303 d128b1@1313 tz0b0@1323 sL8b1@1333 Dw0d.8@1343 mq128b1@1354 zb0c0@1394 p0_0b0.4@1424 Z16_0b0@1434 PBf256n@1444 ab384b1@1455 rb256b1@1465 rb384b1@1475 Dw0d.9@1485 p1_128b1@1505 zb2560c1*@1515 xo0x@1525 p1_0b1.3@1535 m01_128b1@1556 p3_0c0@1566 Dw0d.10@1576 p0_0c0@1596 Dw0d.12@1616 Dw0d.13@1626 zb1024c0@1647 pzc0@1657 tz128b1@1667 p1_0b1.4@1687 az64c0@1697 X1_0x.1@1707 zb3584c1*@1717 Dw0d.14@1727 zb3072c1*@1737 pzc0.1@1748 x2_0x@1758 az576c0@1768 p1_0c1@1778 Z16_128b1@1798 pzc0.2@1808 p0_0c0.1@1818 pzc0.3@1828 pzc1@1839 p0_0c0.2@1849 xo128x@1859 az1088c0@1869 p0_64c0@1879 az1600c0@1889 p0_64c0.2@1899 p0_64c0.1@1909 Dx0i@1929 em0e0@1950 dm128b1@1960 pzc1.1@1970 sg2_0c0@1980 Gfe1s@1990 pzc1.3@2000 p0_0c0.3@2010 p3_0c0.1@2020 p0_0e0@2031 pzc1.2@2041 X0_0x@2051 az2112c1@2061 p1_0c1.1@2071 lte0e0@2081 az2624c1@2091 az3136c1@2101 cle1s@2111 az3648c1@2121 p1_0c1.2@2142 ea0e0*@2162 X1_0nd@2172 x2_128x*@2202 E0e0@2212 X1_0x@2222 p1_64c1@2243 p1_64c1.1@2253 p1_64c1.2@2263 sg2_128c1@2293 Ds0dd@2313 q2_0e0@2324 G0e0@2334 eL0e0@2344 q0e0@2354 p3_0c1.1@2364 X0_0x.1@2414 p1_0c1.3@2435 em128e1@2465 ac4b0@2485 p1_0e1@2526 p4_500b1@2536 p3_0c1@2556 lte128e1@2566 Eh128e1@2617 yx1024xd@2647 ea128e1*@2677 G256e1@2708 eL8e1@2738 q2_128e1@2829 Dlds@2839 yx0xd@3051 Dx0dd@3081 Gfe0s@3091 Efe1s@3162 Gf1e1@3213 yl0e0d@3829 yl256e1d@3920 yq0e0d@4264 q128e1*@4688 yq128e1d@5274
+"""
 EVEN = 2560.0
 BIG = 8192.0
-PAD = 16
+
+
+def sb(cols, dtype):
+    return ("sbuf", [128, cols], dtype)
+
 
 SCRATCH = {
-    "X": ("sbuf", [128, 2048], "bfloat16"), "G": ("sbuf", [128, 512], "float32"), "Gi": ("sbuf", [128, 512], "int32"),
-    "Gf": ("sbuf", [128, 1536], "float32"), "G0": ("sbuf", [128, 512], "int32"), "X2": ("sbuf", [128, 2048], "bfloat16"),
-    "BOw": ("sbuf", [128, 128], F16), "cn": ("sbuf", [128, 16], F16), "In16": ("sbuf", [128, 128], F16),
-    "ds": ("sbuf", [128, 256], "bfloat16"), "al": ("sbuf", [128, 512], "bfloat16"), "Dg2": ("sbuf", [128, 256], F16),
-    "Dw": ("sbuf", [128, 2064], "int32"), "Ds": ("sbuf", [128, 128], "int32"), "Dl": ("sbuf", [128, 512], "int32"),
-    "Tv": ("sbuf", [128, 2048], "float32"),
-    "xb": ("sbuf", [128, 4096 + 8 * PAD], "bfloat16"), "dl": ("sbuf", [128, 4096 + 8 * PAD], "bfloat16"),
-    "Zr": ("sbuf", [128, 128], "bfloat16"), "I4n": ("sbuf", [128, 128], "bfloat16"), "Wl": ("sbuf", [128, 144], "bfloat16"), "eD": ("sbuf", [128, 16], "uint16"),
-    "vq": ("sbuf", [128, 256], "float32"), "Ef": ("sbuf", [128, 384], F16), "clf": ("sbuf", [128, 48], "uint16"),
-    "rl": ("sbuf", [128, 4096], "bfloat16"), "pm": ("sbuf", [128, 4096], "bfloat16"),
-    "zb": ("sbuf", [128, 4096], "bfloat16"), "az": ("sbuf", [128, 4096], "bfloat16"),
-    "q": ("sbuf", [128, 256], "bfloat16"), "q2": ("sbuf", [128, 256], F16),
-    "Ei": ("sbuf", [128, 256], "int32"), "E": ("sbuf", [128, 256], F16),
-    "wc": ("sbuf", [128, 16], "bfloat16"), "thi": ("sbuf", [128, 4], "int32"), "thf": ("sbuf", [128, 4], "float32"),
-    "ci": ("sbuf", [128, 8], "int32"), "cf": ("sbuf", [128, 16], "float32"), "bs": ("sbuf", [128, 4], "float32"),
-    "Xr": ("sbuf", [128, 144], "float32"), "X16": ("sbuf", [128, 128], "float32"), "Lr": ("sbuf", [128, 256], "bfloat16"),
-    "ai": ("sbuf", [128, 48], "float32"), "bI": ("sbuf", [128, 32], "int32"), "bL": ("sbuf", [128, 16], "bfloat16"),
-    "W": ("sbuf", [128, 144], "bfloat16"), "W2": ("sbuf", [128, 144], "bfloat16"), "Wn": ("sbuf", [128, 144], "bfloat16"),
-    "Ww": ("sbuf", [128, 144], "bfloat16"), "Wh": ("sbuf", [128, 144], F16),
-    "WD0": ("sbuf", [128, 144], F16), "WD1": ("sbuf", [128, 144], F16),
-    "I": ("sbuf", [128, 128], "bfloat16"), "In": ("sbuf", [128, 128], "bfloat16"), "I16": ("sbuf", [128, 128], F16),
-    "I4": ("sbuf", [128, 128], "bfloat16"), "IB": ("sbuf", [128, 128], "bfloat16"), "Sh": ("sbuf", [128, 128], "bfloat16"),
-    "BO": ("sbuf", [128, 128], "bfloat16"), "BO2": ("sbuf", [128, 128], "bfloat16"), "BOn": ("sbuf", [128, 128], "bfloat16"),
-    "BOn2": ("sbuf", [128, 128], "bfloat16"), "Tri": ("sbuf", [128, 128], "bfloat16"), "W15": ("sbuf", [128, 128], "float32"),
-    "E8": ("sbuf", [128, 128], "float32"), "Cm": ("sbuf", [128, 256], "bfloat16"),
-    "km": ("sbuf", [128, 1024], "bfloat16"),
-    "u0": ("sbuf", [128, 16], "int32"), "u": ("sbuf", [128, 16], "int32"), "t1": ("sbuf", [128, 16], "int32"),
-    "t2": ("sbuf", [128, 16], "int32"), "t3": ("sbuf", [128, 16], "int32"), "nI": ("sbuf", [128, 16], "int32"),
-    "ub": ("sbuf", [128, 32], "int32"), "uc": ("sbuf", [128, 32], "int32"),
-    "n16": ("sbuf", [128, 32], "uint16"), "cx16": ("sbuf", [128, 64], "uint16"), "nh": ("sbuf", [128, 32], F16),
-    "cL": ("sbuf", [128, 32], "uint16"), "nd": ("sbuf", [128, 32], "uint16"),
-    "sL": ("sbuf", [128, 16], "uint16"), "eL": ("sbuf", [128, 16], "uint16"),
-    "Dg": ("sbuf", [128, 256], F16), "nr": ("sbuf", [128, 256], "float32"), "Vc": ("sbuf", [128, 256], "float32"),
-    "eq": ("sbuf", [128, 256], "bfloat16"),
-    "P16": ("sbuf", [128, 256], "uint16"), "B16": ("sbuf", [128, 256], "uint16"), "Z16": ("sbuf", [128, 256], "uint16"),
-    "Pf": ("sbuf", [128, 256], F16), "Bf": ("sbuf", [128, 256], F16), "Ih16": ("sbuf", [128, 128], F16),
-    "tz": ("sbuf", [128, 256], F16), "df": ("sbuf", [128, 256], F16), "te": ("sbuf", [128, 256], F16),
-    "sg": ("sbuf", [128, 256], "bfloat16"), "lts": ("sbuf", [128, 256], "bfloat16"), "sg2": ("sbuf", [128, 512], "bfloat16"),
-    "lte": ("sbuf", [128, 256], "bfloat16"), "mq": ("sbuf", [128, 256], "bfloat16"), "d": ("sbuf", [128, 256], "bfloat16"),
-    "dm": ("sbuf", [128, 256], "float32"), "xs": ("sbuf", [128, 256], "bfloat16"), "ys": ("sbuf", [128, 256], "bfloat16"),
-    "mx": ("sbuf", [128, 256], "bfloat16"), "my": ("sbuf", [128, 256], "bfloat16"), "m01": ("sbuf", [128, 256], "bfloat16"),
-    "jk": ("sbuf", [128, 256], "bfloat16"), "ac": ("sbuf", [128, 4], "float32"), "Ac": ("sbuf", [128, 4], "float32"),
-    "xo": ("sbuf", [128, 256], F16), "x2": ("sbuf", [128, 256], "bfloat16"),
+    "X0": sb(2048, BF), "X1": sb(2048, BF), "G": sb(512, F32), "Gi": sb(512, I32), "Gf": sb(1536, F32), "Ga": sb(512, I32),
+    "Dw": sb(2064, I32), "Dx": sb(2048, I32), "Ds": sb(128, I32), "Dl": sb(512, I32), "Tv": sb(2048, F32), "Tc": sb(2048, F32),
+    "xb": sb(4096, BF), "dl": sb(4096, BF), "rl": sb(4096, BF), "pm": sb(4096 + 128, BF), "zb": sb(4096, BF), "az": sb(4096, BF),
+    "q": sb(256, BF), "q2": sb(256, F16), "Ei": sb(256, I32), "E": sb(256, F32), "ea": sb(256, F32), "em": sb(256, F32),
+    "wc": sb(16, BF), "K16": sb(16, F32), "thi": sb(4, I32), "thf": sb(4, F32), "ci": sb(8, I32), "cf": sb(20, F32), "bs": sb(4, F32),
+    "Xr": sb(144, F32), "X16": sb(128, F32), "Lr": sb(256, BF), "ai": sb(16, F32), "bI": sb(32, I32), "bL": sb(16, BF),
+    "W": sb(144, BF), "W2": sb(144, BF), "Wn": sb(144, BF), "Ww": sb(144, BF), "Wh": sb(144, F16),
+    "WD0": sb(144, F16), "WD1": sb(144, F16), "I": sb(128, BF), "In": sb(128, BF), "I16": sb(128, F16), "In16": sb(128, F16),
+    "Ih16": sb(128, F16), "Ihn": sb(128, F16), "I4": sb(128, BF), "Sh": sb(128, BF), "BO": sb(128, BF), "BO2": sb(128, BF),
+    "BOn": sb(128, BF), "BOn2": sb(128, BF), "T8": sb(128, BF), "T8n": sb(128, BF), "W15": sb(128, F32), "E8": sb(128, F32),
+    "Cm": sb(256, BF), "BK": sb(512, BF), "km": sb(2048, BF), "jk": sb(256, BF),
+    "u0": sb(16, I32), "u": sb(16, I32), "t1": sb(16, I32), "t2": sb(16, I32), "t3": sb(16, I32), "nI": sb(16, I32),
+    "ub": sb(32, I32), "uc": sb(32, I32), "n16": sb(16, U16), "cx16": sb(64, U16), "nh": sb(16, F16),
+    "cL": sb(32, U16), "nd": sb(32, U16), "sL": sb(16, U16), "eL": sb(16, U16),
+    "Dg": sb(256, F16), "Dg2": sb(256, F16), "nr": sb(256, F32), "Vc": sb(256, F32), "eq": sb(256, BF),
+    "PB": sb(512, U16), "PBf": sb(512, F16), "Mg": sb(256, BF), "Z16": sb(256, U16), "tz": sb(256, F16),
+    "sg": sb(256, BF), "lts": sb(256, BF), "sg2": sb(256, BF), "lte": sb(256, BF), "mq": sb(256, BF), "d": sb(256, BF),
+    "dm": sb(256, F32), "ab": sb(512, BF), "rb": sb(512, BF), "m01": sb(256, BF), "ac": sb(8, F32),
+    "Eh": sb(256, F16), "Ef": sb(768, F16), "clf": sb(48, U16), "xo": sb(256, F16), "x2": sb(256, BF),
 }
 for _b in range(8):
-    SCRATCH["p%d" % _b] = ("psum", [128, 512], "float32")
-NDS = 70
-SEMAPHORES = ["V", "S", "P", "G"] + ["m%d" % i for i in range(NDS)] + ["a%d" % i for i in range(28)]
+    SCRATCH["p%d" % _b] = ("psum", [128, 512], F32)
+SEMAPHORES = ["V", "S", "P", "G"] + ["m%d" % i for i in range(70)] + ["a%d" % i for i in range(30)]
 IO = {"xr": 2, "lg": 4, "dr": 4, "qd": 2, "e0": 4, "wt": 2, "th": 4, "yl": 4, "yx": 2, "yq": 2}
-SIZE = {"float32": 4, "int32": 4, "bfloat16": 2, "float16": 2, "uint16": 2}
-COST = {"cyc": 1.0, "pe": 0.5, "fix": 60.0, "wake": 80.0, "gat": 1.56, "sca": 3.8, "tt2": 1.0, "dma": 2000.0, "rem": 2500.0,
-        "issue": 600.0, "lbw": 150.0, "rbw": 50.0}
+SIZE = {F32: 4, I32: 4, BF: 2, F16: 2, U16: 2}
+COST = {"cyc": 0.92, "pe": 0.5, "fix": 60.0, "wake": 80.0, "gat": 1.56, "sca": 3.8, "tt2": 1.0, "dma": 1700.0, "rem": 2200.0,
+        "issue": 600.0, "lbw": 150.0, "rbw": 50.0, "dq": 100.0}
 A_ = AluOpType
 F_ = ActivationFunctionType
 
@@ -119,7 +106,7 @@ def regions(a):
     if in_psum(a):
         return [(a[1], 0, 512)]
     if a[1] == "Dw":
-        return [("Dw%d" % r, a[2], a[3]) for r in (0, 1) if a[5] is None or a[5][0] == r]
+        return [("Dwr%d" % r, a[2], a[3]) for r in (0, 1) if a[5] is None or a[5][0] == r]
     return [(a[1], a[2], a[3])]
 
 
@@ -133,9 +120,17 @@ def real(T, a):
     return t[r, a[2]:a[3]] if a[4] == 1 else t[r, a[2]:a[3]:a[4]]
 
 
+def pieces(lo, hi, size):
+    return [(s, min(s + size, hi)) for s in range(lo, hi, size)]
+
+
+def cuts(lo, sizes):
+    return [(lo + sum(sizes[:i]), lo + sum(sizes[:i + 1])) for i in range(len(sizes))]
+
+
 def build(cfg, K):
     ops = []
-    where = ["i", "a"]
+    where = ["i"]
 
     def add(eng, calls, occ, lat, kind="c", extra=None):
         rd, wr = [], []
@@ -150,9 +145,8 @@ def build(cfg, K):
                 (wr if out or in_psum(a) else rd).extend(regions(a))
         a = extra[0] if kind == "send" else calls[0][1][0]
         a = a[1] if a[0] == "ind" else a
-        key = "%s%s%d%s" % (eng, a[1], a[2] % 512 if a[1] == "Gf" else a[2], where[0])
-        ops.append({"eng": eng, "calls": calls, "occ": occ, "lat": lat, "kind": kind, "rd": rd, "wr": wr, "x": extra, "key": key,
-                    "grp": where[0] + where[1]})
+        ops.append({"eng": eng, "calls": calls, "occ": occ, "lat": lat, "kind": kind, "rd": rd, "wr": wr, "x": extra,
+                    "key": "%s_%d" % (a[1], a[2]) if a[1][-1] in "0123456789" else "%s%d" % (a[1], a[2]), "grp": where[0]})
 
     def ecost(m, args):
         aps = [a for a in args if is_ap(a) and (a[0] == "ind" or count(a) > 1 or a is args[0])]
@@ -169,8 +163,8 @@ def build(cfg, K):
                 c = n
             else:
                 c = n * (0.5 if two else 1.0)
-            c = max(c, 64 - K["fix"])
-        return K["fix"] + c * K["cyc"]
+            c = max(c, K.get("min", 0))
+        return (K.get("sfix", K["fix"]) if m == "activation" else K["fix"]) + c * K["cyc"]
 
     def V(m, *args):
         c = ecost(m, args)
@@ -179,11 +173,11 @@ def build(cfg, K):
     def tt(o, a, b, op):
         V("tensor_tensor", o, a, b, op)
 
-    def ts(o, a, s1, op0, s2=None, op1=None):
-        if op1 is None:
-            V("tensor_scalar", o, a, s1, None, op0)
-        else:
-            V("tensor_scalar", o, a, s1, s2, op0, op1)
+    def tsargs(o, a, s1, op0, s2=None, op1=None):
+        return (o, a, s1, None, op0) if op1 is None else (o, a, s1, s2, op0, op1)
+
+    def ts(*args):
+        V("tensor_scalar", *tsargs(*args))
 
     def cp(o, a):
         V("tensor_copy", o, a)
@@ -192,11 +186,32 @@ def build(cfg, K):
         c = ecost("activation", (o, a))
         add("S", [("activation", (o, a, f), kw)], c, c)
 
-    def either(o, a, relu=False):
-        act(o, a, F_.Relu if relu else F_.Copy)
-        call = ("tensor_scalar", (o, a, 0.0, None, A_.max), {}) if relu else ("tensor_copy", (o, a), {})
-        c = ecost(call[0], call[1])
-        ops[-1]["alt"] = {"eng": "V", "calls": [call], "occ": c, "lat": c}
+    def alt(m, *args):
+        c = ecost(m, args)
+        ops[-1]["alt"] = {"eng": "V", "calls": [(m, args, {})], "occ": c, "lat": c}
+
+    def gather(o, a):
+        act(o, a, F_.Copy)
+        alt("tensor_copy", o, a)
+
+    def relu(o, a, bias=None):
+        if bias is None:
+            act(o, a, F_.Relu)
+            alt("tensor_scalar", *tsargs(o, a, 0.0, A_.max))
+        else:
+            act(o, a, F_.Relu, bias=bias)
+            alt("tensor_scalar", *tsargs(o, a, bias, A_.add, 0.0, A_.max))
+
+    def nought(o, a):
+        act(o, a, F_.Relu, scale=-1.0, bias=1.0)
+        alt("tensor_scalar", *tsargs(o, a, 0.5, A_.is_lt))
+
+    def affine(o, a, f, b=0.0):
+        act(o, a, F_.Identity, scale=f, bias=b)
+        alt("tensor_scalar", *tsargs(o, a, f, A_.mult, b, A_.add))
+
+    def halved(o, a):
+        affine(o, a, 0.5, -EVEN / 2)
 
     def mm(group, start=True, stop=True):
         calls, c = [], 0.0
@@ -206,22 +221,24 @@ def build(cfg, K):
             o, l, r = e
             calls.append(("matmul", (o, l, r, start if i == 0 else group[i - 1] is None,
                                      stop if i == len(group) - 1 else group[i + 1] is None), {}))
-            c += max(min(64, count(l)), count(r)) * (4 if width(r) == 4 else 1) * K["pe"]
+            c += max(min(64, count(l)), count(r)) * (4 if width(r) == 4 else 1) * K["pe"] + K.get("pfix", 0)
         add("P", calls, c, c + K["fix"])
 
     def iota(o, pat, base, cm):
-        kw = {} if SCRATCH[o[1]][2] == "int32" else {"allow_small_or_imprecise_dtypes": True}
+        kw = {} if SCRATCH[o[1]][2] == I32 else {"allow_small_or_imprecise_dtypes": True}
         c = 130 + 2 * count(o) * K["cyc"]
         add("G", [("iota", (o, pat, base, cm), kw)], c, c)
 
     def dma(o, i, nbytes, eng="Y"):
-        add(eng, [("dma_start", (o, i), {})], 100.0, K["dma"] + nbytes / K["lbw"], "dma")
+        add(eng, [("dma_start", (o, i), {})], K["dq"], K["dma"] + nbytes / K["lbw"], "dma")
+        ops[-1]["flow"] = nbytes / K["lbw"]
 
     def send(o, i, back):
         nb = 128 * count(i) * width(i)
         add("G", [("remote", (None, i), {})], K["issue"], K["issue"] + 1000 + nb / K["rbw"], "send", (o, back))
+        ops[-1]["flow"] = nb / K["rbw"]
         ops.append({"eng": None, "calls": [], "occ": 0.0, "lat": K["rem"] + nb / K["rbw"], "kind": "arr", "rd": [],
-                    "wr": regions(o), "x": len(ops) - 1})
+                    "wr": regions(o), "x": len(ops) - 1, "key": "arr", "grp": where[0]})
 
     def sel(name, k):
         return ap(name, 15 - k, 143 - k)
@@ -229,375 +246,373 @@ def build(cfg, K):
     def col(name, j):
         return ap(name, j, j + 1)
 
+    def tolist(o, w, name, j0, j1, first=()):
+        mm(list(first) + [(o, sel(w, l), ap(name, j0 + l, j1, 16)) for l in range(16)])
+
     CH = cfg["CH"]
-    J = [sum(CH[:i]) for i in range(len(CH) + 1)]
+    nch = len(CH)
+    J = [sum(CH[:i]) for i in range(nch + 1)]
+    CB = ["p0", "p1", "p2", "p3"][:nch]
+    CC = ["p3" if cfg["CC"][c] else CB[c] for c in range(nch)]
+    ZB, zn = ["p5", "p6"] + [b for b in ("p2", "p3") if b not in CB + CC], [0]
+    book0, book1 = ap("Dw", 0, 2048, 1, (0, 128, 16)), ap("Dw", 0, 2048, 1, (1, 128, 16))
     dma(ap("q"), ap("qd"), 65536)
     dma(col("wc", 0), ap("wt"), 4096, "S")
+    dma(ap("Ds"), ap("dr"), 65536)
     dma(ap("Gi", 0, 256), ap("lg", 0, 256), 131072, "S")
     dma(ap("Gi", 256, 512), ap("lg", 256, 512), 131072, "S")
-    dma(ap("Ds"), ap("dr"), 65536)
     dma(ap("thi", 0, 2, 1, (0, 8)), ap("th"), 1024, "S")
-    for m0 in range(0, 2064, 688):
-        V("memset", ap("Dw", m0, m0 + 688), 0)
-    dma(ap("Dw", 0, 2048, 1, (0, 128, 16)), ap("dr"), 65536)
-    dma(ap("X"), ap("xr"), 524288)
-    dma(ap("Ei"), ap("e0"), 131072, "S")
     iota(col("ci", 0), [[0, 1]], 0, 1)
     iota(ap("Xr"), [[1, 144]], 0, 0)
+    dg = cfg["DG"]
+    if dg:
+        iota(ap("Dw", 0, dg), [[0, dg]], 0, 0)
+    for (m0, m1) in pieces(dg, 2064, 520):
+        V("memset", ap("Dw", m0, m1), 0)
+    dma(book0, ap("dr"), 65536)
+    dma(ap("X0"), ap("xr"), 524288)
+    dma(ap("Ei"), ap("e0"), 131072, "S")
     ts(col("ci", 1), col("ci", 0), 112, A_.bitwise_and)
     ts(col("ci", 2), col("ci", 0), 15, A_.bitwise_and)
     cp(ap("cf", 0, 3), ap("ci", 0, 3))
     pc, gc, kc = col("cf", 0), col("cf", 1), col("cf", 2)
     ts(ap("W"), ap("Xr"), gc, A_.subtract, 15.0, A_.is_equal)
     ts(ap("Ww"), ap("W"), col("wc", 0), A_.mult)
-    cp(ap("G"), ap("Gi"))
     send(ap("Dl", 0, 128), ap("Ds"), 1)
-    send(ap("G0", 0, 256), ap("Gi", 0, 256), 1)
-    send(ap("G0", 256, 512), ap("Gi", 256, 512), 1)
-    ts(col("cf", 3), kc, 0.0, A_.is_equal)
-    ts(col("cf", 4), kc, 1.0, A_.is_equal)
-    ts(col("cf", 5), kc, 15.0, A_.is_equal)
-    ts(col("cf", 6), kc, 15.0, A_.not_equal)
-    ts(col("cf", 7), kc, -1.0, A_.mult)
-    ts(col("cf", 8), kc, 2048.0, A_.add)
-    ts(col("cf", 9), pc, 16.0, A_.mult)
-    ts(col("cf", 10), col("cf", 3), -BIG, A_.mult, -0.5, A_.add)
-    ts(ap("WD0"), ap("W"), col("cf", 3), A_.mult)
-    ts(ap("WD1"), ap("W"), col("cf", 4), A_.mult)
-    ts(ap("Wh"), ap("Ww"), 0.5, A_.mult)
-    for (o, s, f) in (("W2", "W", 2.0), ("Wn", "W", -1.0)):
-        act(ap(o), ap(s), F_.Identity, scale=f)
+    send(ap("Ga", 0, 256), ap("Gi", 0, 256), 1)
+    send(ap("Ga", 256, 512), ap("Gi", 256, 512), 1)
+    ts(ap("K16"), ap("Xr", 0, 16), kc, A_.is_equal)
+    k0, k1, k15 = col("K16", 0), col("K16", 1), col("K16", 15)
+    affine(col("cf", 7), k15, -1.0, 1.0)
+    affine(col("cf", 8), kc, 1.0, 2048.0)
+    affine(col("cf", 9), pc, 16.0)
+    affine(col("cf", 10), k0, -BIG)
+    affine(ap("WD0"), ap("W"), k0)
+    affine(ap("WD1"), ap("W"), k1)
+    affine(ap("Wh"), ap("Ww"), 0.5)
+    if not all(cfg["AB"]) or any(cfg["AV"]):
+        affine(ap("W2"), ap("W"), 2.0)
+        affine(ap("Wn"), ap("W"), -1.0)
     x128 = ap("Xr", 0, 128)
     ts(ap("I"), x128, pc, A_.is_equal)
-    cp(ap("I16"), ap("I"))
     iota(ap("X16"), [[16, 8], [0, 16]], 0, 0)
     ts(ap("BO"), ap("X16"), gc, A_.is_equal)
-    for (o, s, f) in (("In", "I", -1.0), ("I4", "I", 4096.0), ("IB", "I", -BIG), ("BO2", "BO", 2.0), ("BOn", "BO", -1.0),
-                      ("BOn2", "BO", -2.0)):
-        act(ap(o), ap(s), F_.Identity, scale=f)
-    ts(ap("BOw"), ap("BO"), col("wc", 0), A_.mult, 0.5, A_.mult)
-    ts(ap("In16"), ap("I"), -1.0, A_.mult)
-    if not cfg["MV"]:
-        ts(ap("Ih16"), ap("I"), 0.5, A_.mult)
-    V("memset", ap("jk", 0, 16), -EVEN)
-    cp(ap("cn"), ap("jk", 0, 16))
-    ts(ap("jk", 0, 128), x128, pc, A_.is_ge)
-    tt(ap("Tri"), ap("jk", 0, 128), ap("BO"), A_.mult)
+    for (o, s, f) in (("In", "I", -1.0), ("I4", "I", 4096.0), ("BO2", "BO", 2.0), ("BOn", "BO", -1.0), ("BOn2", "BO", -2.0),
+                      ("I16", "I", 1.0), ("In16", "I", -1.0), ("Ih16", "I", 0.5)) + ((("Ihn", "I", -0.5),) if any(cfg["MP"]) else ()):
+        affine(ap(o), ap(s), f)
+    ts(ap("jk", 0, 128), x128, pc, A_.is_ge, BIG, A_.mult)
+    tt(ap("T8"), ap("jk", 0, 128), ap("BO"), A_.mult)
+    affine(ap("T8n"), ap("T8"), -1.0)
     ts(ap("jk", 128, 256), x128, pc, A_.subtract, 1.0, A_.is_equal)
-    ts(ap("Sh"), ap("jk", 128, 256), col("cf", 6), A_.mult, -BIG, A_.mult)
-    ts(ap("W15"), x128, -1.0, A_.is_ge, col("cf", 5), A_.mult)
+    affine(col("cf", 17), k15, BIG, -BIG)
+    affine(ap("Sh"), ap("jk", 128, 256), col("cf", 17))
+    affine(col("cf", 11), k15, 16.0)
+    affine(ap("W15"), x128, 0.0, col("cf", 11))
     ts(ap("E8"), ap("X16"), col("cf", 9), A_.is_equal)
     cp(ap("thf", 0, 2, 1, (0, 8)), ap("thi", 0, 2, 1, (0, 8)))
-    mm([(ap("p2", 0, 2), ap("E8", 0, 128, 1, (0, 8)), ap("thf", 0, 2, 1, (0, 8)))])
-    ts(col("bs", 2), ap("p2", 0, 1), -1.0, A_.mult, -0.5, A_.add)
-    ts(col("bs", 1), ap("p2", 1, 2), -1.0, A_.mult, col("cf", 10), A_.add)
-    ts(col("bs", 0), col("bs", 2), col("cf", 6), A_.mult, col("cf", 5), A_.add)
-    iota(ap("ai", 0, 16), [[16, 16]], 0, 0)
-    ts(ap("ai", 16, 32), ap("ai", 0, 16), kc, A_.add)
-    ts(ap("bL"), ap("ai", 16, 32), 16.0, A_.mult)
-    ts(ap("bI", 16, 32), ap("ai", 16, 32), 8.0, A_.mult)
-    for c in range(len(CH)):
-        ts(ap("bI", J[c] // 16, J[c + 1] // 16), ap("ai", 16 + J[c] // 16, 16 + J[c + 1] // 16), 2.0, A_.mult,
-           -2.0 * J[c], A_.add)
-    V("memset", ap("km"), 1.0)
-    V("memset", ap("km", 0, 1024, 16), 0.0)
-    XO = [16 * J[c] + PAD * (c + 1) for c in range(len(CH))]
-    for c in range(len(CH)):
-        V("memset", ap("xb", XO[c] - PAD, XO[c]), 0.0)
-        if cfg["P2"][c]:
-            V("memset", ap("dl", XO[c] + 16 * CH[c], XO[c] + 16 * CH[c] + PAD), 0.0)
-    if any(cfg["P2"]):
-        act(ap("I4n"), ap("I"), F_.Identity, scale=-4096.0)
-        V("memset", ap("Zr"), 0.0)
-        ts(ap("Wl"), ap("W"), col("cf", 5), A_.mult, -4096.0, A_.mult)
-        ts(col("bs", 3), col("bs", 1), -4096.0, A_.add)
+    mm([(ap("p3", 0, 2), ap("E8", 0, 128, 1, (0, 8)), ap("thf", 0, 2, 1, (0, 8))), None, (ap("p3", 2, 3), ap("BO"), col("wc", 0))])
+    affine(col("bs", 2), ap("p3", 0, 1), -1.0)
+    affine(col("bs", 1), ap("p3", 1, 2), -1.0, col("cf", 10))
+    affine(col("bs", 3), ap("p3", 2, 3), -EVEN / 2)
+    affine(col("bs", 0), col("bs", 2), col("cf", 7), k15)
+    for m in (0, 1024):
+        iota(ap("Tv", m, m + 1024), [[1, 1024]], m, 0)
+        iota(ap("Tc", m, m + 1024), [[2, 128], [0, 4], [1, 2]], m // 4, 0)
+        if cfg["D3"]:
+            iota(ap("Dx", m, m + 1024), [[0, 1024]], 0, 0)
+    affine(ap("ai"), ap("Xr", 0, 16), 16.0, kc)
+    affine(ap("bL"), ap("ai"), 16.0)
+    ts(ap("bI", 16, 32), ap("ai"), 8.0, A_.mult)
+    for c in range(nch):
+        ts(ap("bI", J[c] // 16, J[c + 1] // 16), ap("ai", J[c] // 16, J[c + 1] // 16), 2.0, A_.mult, -2.0 * J[c], A_.add)
+    nk = 16 * max(cfg["SC"])
+    V("memset", ap("km", 0, nk), 1.0)
+    V("memset", ap("km", 15, nk, 16), 0.0)
+    PO = [16 * J[c] + 16 * c for c in range(nch)]
+    for c in range(nch):
+        V("memset", col("pm", PO[c]), 0.0)
     V("memset", ap("nd"), 0)
-    cp(ap("E"), ap("Ei"))
+    cp(ap("G"), ap("Gi"))
+
+    def banks(u):
+        per = 512 // u
+        return [list(range(k, min(k + per, 16))) for k in range(1, 16, per)]
+    BK = {}
+    for c in range(nch):
+        if cfg["AV"][c]:
+            kb0 = banks(cfg["U2"][c])[-cfg["AV"][c]][0]
+            if kb0 not in BK:
+                BK[kb0] = ap("BK", 128 * len(BK), 128 * len(BK) + 128)
+                ts(ap("jk", 0, 128), x128, gc, A_.subtract, float(kb0), A_.is_ge)
+                tt(BK[kb0], ap("jk", 0, 128), ap("BO"), A_.mult)
     iota(ap("Lr"), [[0, 16], [1, 16]], 0, 0)
     ts(ap("Cm"), ap("Lr"), kc, A_.is_ge, 4096.0, A_.mult)
-    iota(ap("Tv"), [[1, 2048]], 0, 0)
-    ops[-1]["aft"] = [i for i, o in enumerate(ops[:-1]) if o["eng"] == "G"]
 
-    Xw = ap("X")
     for t in range(STEPS):
         last = t == STEPS - 1
-        o16, o32 = 16 * (t % 2), 32 * (t % 2)
-        Gf = ap("Gf", 512 * t - 512, 512 * t) if t else ap("G0")
-        NG = cfg["NG"] if t else [0, len(CH)]
-        cLo = {}
-        where[0], where[1] = "n", "a"
+        o32 = 32 * (t % 2)
+        Gw = ap("G") if t else ap("Gi")
+        Gf = ap("Gf", 512 * t - 512, 512 * t) if t else ap("Ga")
+        Xw, Xn = ap("X0"), ap("X1" if last else "X0")
+        NG = cfg["NG"]
+        groups = [(J[NG[gi]], J[NG[gi + 1]]) for gi in range(len(NG) - 1)]
+        where[0] = "n%d" % t
         if last:
-            dma(ap("X2"), Xw, 524288)
-        for gi in range(len(NG) - 1):
-            j0, j1 = J[NG[gi]], J[NG[gi + 1]]
+            dma(Xn, Xw, 524288)
+        late = []
+        for gi, (j0, j1) in enumerate(groups):
             a0, a1 = j0 // 16, j1 // 16
             na = a1 - a0
 
-            def L(name, o=0):
-                return ap(name, o + a0, o + a1)
-            if t == 0:
-                mm([(ap("p7", 0, na), sel("Ww", l), ap("q", j0 + l, j1, 16)) for l in range(16)])
+            def L(name):
+                return ap(name, a0, a1)
+            nb = CB[-1] if gi else "p7"
+            if t == 0 and gi == 0:
+                a1 = 16
+                tolist(ap(nb, 0, 16), "Ww", "q", 0, C)
+                cp(L("u0"), ap(nb, 0, 16))
+            elif t:
+                tolist(ap(nb, 0, na), "Wh", "q2", j0, j1)
+                ts(L("u0"), ap(nb, 0, na), col("bs", 3), A_.add)
+            ops[-2]["key"] = "pu%d" % gi if t or gi == 0 else ops[-2]["key"]
+            if t or gi == 0:
+                ts(L("u"), L("u0"), 2047, A_.bitwise_and)
+                tt(L("t2"), L("u"), L("u"), A_.mult)
+                if t:
+                    ts(L("t1"), L("u"), 1184.0, A_.mult, col("p4", 500), A_.add)
+                else:
+                    ts(L("t1"), L("u"), 1184.0, A_.mult)
+                tt(L("t3"), L("t1"), L("t2"), A_.add)
+                ts(L("nI"), L("t3"), 5, A_.arith_shift_right, 2047, A_.bitwise_and)
+                cp(L("n16"), L("nI"))
+            a1 = j1 // 16
+            gather(ap("Dg", j0, j1), ind(ap("Dw", 0, 2048), L("n16")))
+            tolist(ap(nb, 0, na), "WD0", "Dg", j0, j1)
+            ops[-1]["key"] = "pc%d" % gi
+            cp(ap("cL", 2 * a0, 2 * a0 + na), ap(nb, 0, na))
+            if t == 0 or cfg["D2"][gi] or cfg["D3"]:
+                late.append(gi)
             else:
-                mm([(ap("p7", 0, na), ap("BOw"), ap("cn", 0, na))] +
-                   [(ap("p7", 0, na), sel("Wh", l), ap("q2", j0 + l, j1, 16)) for l in range(16)])
-            cp(L("u0"), ap("p7", 0, na))
-            ts(L("u"), L("u0"), 2047, A_.bitwise_and)
-            ts(L("t1"), L("u"), 1184.0, A_.add)
-            tt(L("t2"), L("t1"), L("u"), A_.mult)
-            src = "t2"
-            if t > 0:
-                ts(L("t3"), L("t2"), col("Ac", 0), A_.add)
-                src = "t3"
-            ts(L("nI"), L(src), 5, A_.arith_shift_right, 2047, A_.bitwise_and)
-            cp(L("n16", o16), L("nI"))
-            if not last:
-                cp(L("nh", o16), L("nI"))
-            cp(ap("Dg", j0, j1), ind(ap("Dw", 0, 2048), L("n16", o16)))
-            mm([(ap("p7", 0, na), sel("WD0", l), ap("Dg", j0 + l, j1, 16)) for l in range(16)])
-            if t == 0:
-                cp(ap("cL", 0, 16), ap("p7", 0, 16))
-                dma(ap("Dw", 0, 2048, 1, (1, 128, 16)), ap("Dl", 0, 128), 65536)
-                cp(ap("Dg2"), ind(ap("Dw", 0, 2048), L("n16", o16)))
-                mm([(ap("p4", 0, 16), sel("WD1", l), ap("Dg2", l, 256, 16)) for l in range(16)])
-                cp(ap("cL", 16, 32), ap("p4", 0, 16))
-            elif gi == 0 and cfg["oc"]:
-                cp(ap("cL", 2 * a0, 2 * a0 + na), ap("p7", 0, na))
-                mm([(ap("p7", na, 2 * na), sel("WD1", l), ap("Dg", j0 + l, j1, 16)) for l in range(16)])
-                cp(ap("cL", 2 * a0 + na, 2 * a1), ap("p7", na, 2 * na))
+                ob = "p7" if gi else CB[0]
+                tolist(ap(ob, 0, na), "WD1", "Dg", j0, j1)
+                ops[-1]["key"] = "po%d" % gi
+                cp(ap("cL", 2 * a0 + na, 2 * a1), ap(ob, 0, na))
+            if (t == 0 and gi == len(groups) - 1) or (t and gi == 0 and cfg["D2"][0]):
+                dma(book1, ap("Dl", 128 * t, 128 * t + 128), 65536)
+        for gi in late:
+            j0, j1 = groups[gi]
+            a0, a1 = j0 // 16, j1 // 16
+            gather(ap("Dg2", j0, j1), ind(ap("Dx" if cfg["D3"] and t else "Dw", 0, 2048), ap("n16", a0, a1)))
+            ob = "p7" if gi else CB[0]
+            tolist(ap(ob, 0, a1 - a0), "WD1", "Dg2", j0, j1)
+            ops[-1]["key"] = "po%d" % gi
+            cp(ap("cL", a0 + a1, 2 * a1), ap(ob, 0, a1 - a0))
+        Pn, Bn = {}, {}
+        for gi, (j0, j1) in enumerate(groups):
+            a0, a1 = j0 // 16, j1 // 16
+            both = ((2 * j0, j0 + j1, ind(Gw, ap("cL", 2 * a0, a0 + a1))), (j0 + j1, 2 * j1, ind(Gf, ap("cL", a0 + a1, 2 * a1))))
+            if cfg["PS"][gi]:
+                for (c0, c1, src) in both:
+                    gather(ap("PBf", c0, c1), src)
+                    cp(ap("PB", c0, c1), ap("PBf", c0, c1))
             else:
-                mm([(ap("p7", na, 2 * na), sel("WD1", l), ap("Dg", j0 + l, j1, 16)) for l in range(16)])
-                cp(ap("cL", 2 * a0, 2 * a1), ap("p7", 0, 2 * na))
+                for (c0, c1, src) in both:
+                    cp(ap("PB", c0, c1), src)
+                cp(ap("PBf", 2 * j0, 2 * j1), ap("PB", 2 * j0, 2 * j1))
             for c in range(NG[gi], NG[gi + 1]):
-                cLo[c] = (a0 + J[c] // 16, a0 + J[c] // 16 + na)
-            ts(L("ub"), L("u0"), 1, A_.bitwise_and)
-            ts(L("ub", 16), L("u0"), 7, A_.bitwise_and)
+                Pn[c], Bn[c] = j0, j1
+        ts(ap("ub", 0, 16), ap("u0"), 1, A_.bitwise_and)
+        ts(ap("ub", 16, 32), ap("u0"), 7, A_.bitwise_and)
         tt(ap("uc"), ap("ub"), ap("bI"), A_.add)
         cp(ap("cx16", o32, o32 + 32), ap("uc"))
-        for gi in range(len(cfg["PG"]) - 1):
-            c = cfg["PG"][gi]
-            j0, j1 = J[c], J[cfg["PG"][gi + 1]]
-            na = (j1 - j0) // 16
-            cp(ap("P16", j0, j1), ind(ap("G"), ap("cL", cLo[c][0], cLo[c][0] + na)))
-            cp(ap("B16", j0, j1), ind(Gf, ap("cL", cLo[c][1], cLo[c][1] + na)))
-            cp(ap("Pf", j0, j1), ap("P16", j0, j1))
-            cp(ap("Bf", j0, j1), ap("B16", j0, j1))
-        where[1] = "d"
+        cxl = ap("cx16", o32 + 16, o32 + 32)
+        where[0] = "d%d" % t
         if not last:
-            either(ap("nr"), ind(ap("Tv"), ap("n16", o16, o16 + 16)))
-            for c in range(len(CH)):
-                either(ap("Vc", J[c], J[c + 1]), ind(ap("Tv", 2 * J[c], 2 * J[c + 1]), ap("cx16", o32 + J[c] // 16, o32 + J[c + 1] // 16)))
-            mm([(ap("p7", 0, 256), ap("I"), ap("Cm"))] +
-               [(ap("p7", l, 256, 16), ap("I16"), ap("nh", o16, o16 + 16)) for l in range(16)])
-            tt(ap("eq"), ap("nr"), ap("p7", 0, 256), A_.is_equal)
-            mm([(ap("p7", 0, 16), ap("I16"), ap("nh", o16, o16 + 16))] +
-               [(ap("p7", 0, 16), ap("I4"), ap("eq", l, 256, 16)) for l in range(15)])
-            ts(ap("nd", 0, 32, 2), ap("p7", 0, 16), col("cf", 8), A_.min)
+            cp(ap("nh"), ap("nI"))
+            gather(ap("nr"), ind(ap("Tv"), ap("n16")))
+            gather(ap("Vc"), ind(ap("Tc"), cxl))
+            mm([(ap("p4", 0, 256), ap("I"), ap("Cm"))] + [(ap("p4", l, 256, 16), ap("I16"), ap("nh")) for l in range(16)])
+            tt(ap("eq"), ap("nr"), ap("p4", 0, 256), A_.is_equal)
+            mm([(ap("p4", 0, 16), ap("I16"), ap("nh"))] + [(ap("p4", 0, 16), ap("I4"), ap("eq", l, 256, 16)) for l in range(15)])
+            ts(ap("nd", 0, 32, 2), ap("p4", 0, 16), col("cf", 8), A_.min)
             for a in range(15, -1, -1):
                 cp(ind(ap("Dw"), ap("nd", 2 * a, 2 * a + 1)), ap("Vc", 16 * a, 16 * a + 16))
-            dma(ap("Ds"), ap("Dw", 0, 2048, 1, (0, 128, 16)), 65536)
+            dma(ap("Ds"), book0, 65536)
             send(ap("Dl", 128 * t + 128, 128 * t + 256), ap("Ds"), t + 2)
-            dma(ap("Dw", 0, 2048, 1, (1, 128, 16)), ap("Dl", 128 * t + 128, 128 * t + 256), 65536)
-        SUB = cfg["SUB"]
-        for c in range(len(CH)):
-            j0, j1, nc = J[c], J[c + 1], CH[c]
-            a0, a1, na = j0 // 16, j1 // 16, CH[c] // 16
-            b0, b1, xo = 16 * j0, 16 * j1, XO[c] - 16 * j0
-            where[0], where[1] = "c%d" % c, "a"
-
-            def Kc(name):
-                return ap(name, j0, j1)
-            subs = [(s, min(s + SUB, j1)) for s in range(j0, j1, SUB)]
-            for si, (s0, s1) in enumerate(subs):
-                xs_ = ap("xb", xo + 16 * s0, xo + 16 * s1)
-                either(xs_, ind(Xw, ap("P16", s0, s1)))
-                dl_ = ap("dl", xo + 16 * s0, xo + 16 * s1)
-                if cfg["YS"][c]:
-                    either(dl_, ind(Xw, ap("B16", s0, s1)))
-                    o = ap("p%d" % (5 + si % 2), 0, 16 * (s1 - s0))
-                    mm([(o, ap("In"), xs_), (o, ap("I"), dl_)])
-                    act(ap("rl", 16 * s0, 16 * s1), o, F_.Abs)
-                    continue
-                tt(dl_, ind(Xw, ap("B16", s0, s1)), xs_, A_.subtract)
-                if cfg["ABS"][c]:
-                    act(ap("rl", 16 * s0, 16 * s1), dl_, F_.Abs)
+            if cfg["D3"]:
+                dma(ap("Dx", 0, 2048, 1, (1, 128, 16)), ap("Dl", 128 * t + 128, 128 * t + 256), 65536)
+            elif not cfg["D2"][0]:
+                dma(book1, ap("Dl", 128 * t + 128, 128 * t + 256), 65536)
+        for c in range(nch):
+            j0, j1 = J[c], J[c + 1]
+            where[0] = "a%d%d" % (t, c)
+            for (s0, s1) in cuts(j0, cfg["SX"][c]):
+                xs_, dl_, rl_ = [ap(n, 16 * s0, 16 * s1) for n in ("xb", "dl", "rl")]
+                gather(xs_, ind(Xw, ap("PB", Pn[c] + s0, Pn[c] + s1)))
+                tt(dl_, ind(Xw, ap("PB", Bn[c] + s0, Bn[c] + s1)), xs_, A_.subtract)
+                if cfg["AB"][c]:
+                    act(rl_, dl_, F_.Abs)
                 else:
-                    either(ap("rl", 16 * s0, 16 * s1), dl_, True)
-            for s0 in range(b0, b1, cfg["SC"]):
-                s1 = min(s0 + cfg["SC"], b1)
-                V("tensor_tensor_scan", ap("pm", s0, s1), ap("xb", xo + s0 - 1, xo + s1 - 1), ap("km", 0, s1 - s0), 0.0, A_.max, A_.mult)
-        for c in range(len(CH)):
+                    relu(rl_, dl_)
+            for (s0, s1) in pieces(j0, j1, cfg["SC"][c]):
+                o = PO[c] + 16 * (s0 - j0) + 1
+                V("tensor_tensor_scan", ap("pm", o, o + 16 * (s1 - s0)), ap("xb", 16 * s0, 16 * s1), ap("km", 0, 16 * (s1 - s0)),
+                  0.0, A_.max, A_.mult)
+        for c in range(nch):
             j0, j1, nc = J[c], J[c + 1], CH[c]
             a0, a1, na = j0 // 16, j1 // 16, CH[c] // 16
-            b0, b1, xo = 16 * j0, 16 * j1, XO[c] - 16 * j0
-            where[0], where[1] = "c%d" % c, "a"
+            b0, b1 = 16 * j0, 16 * j1
+            where[0] = "b%d%d" % (t, c)
 
             def Kc(name):
                 return ap(name, j0, j1)
-            subs = [(s, min(s + SUB, j1)) for s in range(j0, j1, SUB)]
-            late = cfg["EP"] and c == len(CH) - 1 and not last
-            gf = ap("Gf", 512 * t + 2 * j0, 512 * t + 2 * j1)
-            if late:
-                send(gf, ap("G", 2 * j0, 2 * j1), t + 2)
-                send(ap("clf", 16 * t + a0, 16 * t + a1), ap("cx16", o32 + a0, o32 + a1), t + 2)
-            p0 = ap("p0", 0, nc)
-            if cfg["ABS"][c] or cfg["YS"][c]:
-                mm([(p0, sel("W", k), ap("rl", b0 + k, b1, 16)) for k in range(15)])
-            else:
-                mm([(p0, sel("Wn", k), ap("dl", xo + b0 + k, xo + b1, 16)) for k in range(15)], True, False)
-                mm([(p0, sel("W2", k), ap("rl", b0 + k, b1, 16)) for k in range(15)], False, True)
-            where[1] = "b"
-            pb = "p0" if cfg["ZP"] == 2 else "p1"
-            act(Kc("sg"), p0, F_.Sign, bias=col("bs", 0))
-            mm([(ap(pb, 0, nc), ap("Tri"), Kc("sg"))])
-            act(Kc("lts"), ap(pb, 0, nc), F_.Relu, bias=col("cf", 7), scale=-1.0)
-            mm([(ap(pb, 0, na), ap("I"), ap("bL", 0, na))] +
-               [(ap(pb, 0, na), sel("W", l), ap("lts", j0 + l, j1, 16)) for l in range(16)])
+            P16, B16 = ap("PBf", Pn[c] + j0, Pn[c] + j1), ap("PBf", Bn[c] + j0, Bn[c] + j1)
+            kb = CB[c]
+            p0, pn = ap(kb, 0, nc), ap(kb, nc, 2 * nc)
+            for (u0, u1) in pieces(j0, j1, cfg["U1"][c]):
+                o = ap(kb, u0 - j0, u1 - j0)
+                if cfg["AB"][c]:
+                    mm([(o, sel("W", k), ap("rl", 16 * u0 + k, 16 * u1, 16)) for k in range(15)])
+                else:
+                    mm([(o, sel("Wn", k), ap("dl", 16 * u0 + k, 16 * u1, 16)) for k in range(15)], True, False)
+                    mm([(o, sel("W2", k), ap("rl", 16 * u0 + k, 16 * u1, 16)) for k in range(15)], False, True)
+            relu(Kc("sg"), p0, col("bs", 0))
+            mm([(p0, ap("T8"), Kc("sg"))])
+            nought(Kc("lts"), p0)
+            base = [(ap(kb, 0, na), ap("I"), ap("bL", 0, na))]
+            tolist(ap(kb, 0, na), "W", "lts", j0, j1, base)
             sL = ap("sL", a0, a1)
-            cp(sL, ap(pb, 0, na))
-            tt(Kc("mq"), ind(ap("pm", b0, b1), sL), Kc("q"), A_.subtract)
-            either(Kc("xs"), ind(ap("xb", xo + b0, xo + b1), sL))
-            act(Kc("d"), Kc("mq"), F_.Abs)
-            p2 = ap("p2", 0, nc)
-            if cfg["LS"]:
-                either(Kc("ds"), ind(ap("dl", xo + b0, xo + b1), sL))
-                pn = ap("p2", nc, 2 * nc)
-                mm([(p2, ap("I"), Kc("xs")), (p2, ap("In"), Kc("d")), None,
-                    (pn, ap("I"), Kc("ds")), (pn, ap("In"), Kc("d"))] + ([] if cfg["YS"][c] else [(pn, ap("I"), Kc("xs"))]))
-                act(ap("al", 2 * j0, 2 * j1), ap("p2", 0, 2 * nc), F_.Abs)
-                mm([(pn, ap("I16"), Kc("Bf")), (pn, ap("In16"), Kc("Pf")), None, (p2, ap("IB"), Kc("lts")),
-                    (p2, ap("BO"), ap("al", 2 * j0, 2 * j0 + nc)), (p2, ap("BOn"), ap("al", 2 * j0 + nc, 2 * j1))])
+            cp(sL, ap(kb, 0, na))
+            Mi = ind(ap("pm", PO[c], PO[c] + 16 * nc), sL)
+            if cfg["MP"][c]:
+                gather(Kc("Mg"), Mi)
+                mm([(p0, ap("Ihn"), Kc("q2")) if t else (p0, ap("In"), Kc("q")), (p0, ap("I"), Kc("Mg"))])
+                act(Kc("d"), p0, F_.Abs, bias=EVEN / 2 if t else 0.0)
             else:
-                pn = ap("p2", nc, 2 * nc)
-                if cfg["YS"][c]:
-                    either(Kc("ys"), ind(ap("dl", xo + b0, xo + b1), sL))
+                if t:
+                    halved(Kc("q"), Kc("q2"))
+                tt(Kc("mq"), Mi, Kc("q"), A_.subtract)
+                act(Kc("d"), Kc("mq"), F_.Abs)
+            xa, ya, ab = ap("ab", 2 * j0, j0 + j1), ap("ab", j0 + j1, 2 * j1), ap("ab", 2 * j0, 2 * j1)
+            xr_, yr_, rb = ap("rb", 2 * j0, j0 + j1), ap("rb", j0 + j1, 2 * j1), ap("rb", 2 * j0, 2 * j1)
+            xi, yi = ind(ap("xb", b0, b1), sL), ind(ap("dl", b0, b1), sL)
+            lead = [(pn, ap("I16"), B16), (pn, ap("In16"), P16), None, (p0, ap("I4"), Kc("lts"))]
+            if cfg["LS"][c] == 1:
+                gather(xa, xi)
+                gather(ya, yi)
+                mm([(p0, ap("I"), xa), (p0, ap("In"), Kc("d")), None, (pn, ap("I"), ya), (pn, ap("In"), Kc("d")), (pn, ap("I"), xa)])
+                act(rb, ap(kb, 0, 2 * nc), F_.Abs)
+                mm(lead + [(p0, ap("BOn"), xr_), (p0, ap("BO"), yr_)])
+            else:
+                if cfg["LS"][c] == 2:
+                    tt(xa, xi, Kc("d"), A_.subtract)
+                    tt(ya, yi, xa, A_.add)
+                    relu(rb, ab)
                 else:
-                    tt(Kc("ys"), ind(ap("dl", xo + b0, xo + b1), sL), Kc("xs"), A_.add)
-                tt(Kc("mx"), Kc("xs"), Kc("d"), A_.max)
-                tt(Kc("my"), Kc("ys"), Kc("d"), A_.max)
-                mm([(pn, ap("I16"), Kc("Bf")), (pn, ap("In16"), Kc("Pf")), None,
-                    (p2, ap("IB"), Kc("lts")), (p2, ap("BOn"), Kc("xs")), (p2, ap("BO"), Kc("ys"))], True, False)
-                mm([(p2, ap("BO2"), Kc("mx")), (p2, ap("BOn2"), Kc("my"))], False, True)
-            act(Kc("dm"), Kc("d"), F_.Identity, bias=EVEN - 0.5)
-            if cfg["MV"]:
-                ts(Kc("m01"), p2, 0.0, A_.is_gt)
-            elif last:
-                act(Kc("m01"), p2, F_.Sign, bias=-0.5)
-            else:
-                act(Kc("m01"), p2, F_.Sign, bias=-0.5, accum_out=col("ac", c))
+                    gather(xa, xi)
+                    tt(ya, yi, xa, A_.add)
+                    tt(xr_, xa, Kc("d"), A_.max)
+                    tt(yr_, ya, Kc("d"), A_.max)
+                mm(lead + [(p0, ap("BO"), xa), (p0, ap("BOn"), ya)], True, False)
+                mm([(p0, ap("BOn2"), xr_), (p0, ap("BO2"), yr_)], False, True)
+            affine(Kc("dm"), Kc("d"), 1.0, EVEN - 0.5)
+            kw = {} if last else {"accum_out": col("ac", 5 if c == nch - 1 else c)}
+            act(Kc("m01"), p0, F_.Sign, bias=-0.5, scale=-1.0, **kw)
+            if not last and c == nch - 2:
+                if c:
+                    ts(col("ac", 4), col("ac", 0), col("ac", 1), A_.add, 256.0, A_.add)
+                else:
+                    affine(col("ac", 4), col("ac", 0), 1.0, 256.0)
+            if not last and c == nch - 1:
+                mm([(col("p4", 500), ap("W15"), col("ac", 4)), (col("p4", 500), ap("W15"), col("ac", 5))])
             tt(Kc("tz"), pn, Kc("m01"), A_.mult)
-            df = Kc("df")
 
             def names(o):
-                if cfg["MV"]:
-                    return [(o, ap("I16"), Kc("Pf")), (o, ap("I16"), Kc("tz"))]
-                return [(o, ap("Ih16"), Kc("Pf")), (o, ap("Ih16"), Kc("Bf")), (o, ap("Ih16"), Kc("tz"))]
-            both = cfg["P2"][c] and not cfg["YS"][c]
-            if not both or cfg["ZP"] != 2:
-                mm(names(p2))
-            if not both:
-                cp(Kc("Z16"), p2)
-            if cfg["ZP"] == 2:
-                df = ap("p1", 0, nc)
-                mm([(df, ap("In16"), Kc("E"))] + names(df))
-            else:
-                tt(df, p2, Kc("E"), A_.subtract)
-            if not last and c == len(CH) - 1:
-                if cfg["MV"]:
-                    act(ap("jk"), ap("m01"), F_.Copy, accum_out=col("ac", 0))
-                    mm([(ap("p2", 0, 1), ap("W15"), col("ac", 0))])
-                    act(col("Ac", 0), ap("p2", 0, 1), F_.Identity, scale=32.0)
-                else:
-                    mm([(ap("p2", 0, 1), ap("W15"), col("ac", e)) for e in range(len(CH))])
-                    act(col("Ac", 0), ap("p2", 0, 1), F_.Identity, scale=16.0, bias=32768.0)
-            where[1] = "c"
-            p3 = ap("p3", 0, nc)
-            per = 512 // nc
-            ks = [list(range(k, min(k + per, 16))) for k in range(1, 16, per)]
-            if both:
-                py = ap("p3", nc, 2 * nc)
-                mm([(ap("p3", 0, 2 * nc), ap("Zr"), ap("km", 0, 2 * nc)), (p3, ap("Sh"), Kc("lts")), (py, ap("Sh"), Kc("lts"))], True, False)
+                return [(o, ap("Ih16"), P16), (o, ap("Ih16"), B16), (o, ap("Ih16"), Kc("tz"))]
+            mm(names(p0))
+            cp(Kc("Z16"), p0)
+            where[0] = "c%d%d" % (t, c)
+            shared = CC[c] == kb
+            p1 = pn if shared else ap(CC[c], 0, nc)
+            if not shared:
+                mm(names(p1), True, False)
+            for (s0, s1) in cuts(j0, cfg["SZ"][c]):
+                gather(ap("zb", 16 * s0, 16 * s1), ind(Xw, ap("Z16", s0, s1)))
+            for (u0, u1) in pieces(j0, j1, cfg["U2"][c]):
+                nu = u1 - u0
+                ks = banks(cfg["U2"][c])
+                o3, du = ap(kb, u0 - j0, u1 - j0), ap("d", u0, u1)
+                nv = cfg["AV"][c]
+                mm([(o3, ap("Sh"), ap("lts", u0, u1))] + ([(o3, BK[ks[-nv][0]], du)] if nv else []), True, False)
                 for bi, kk in enumerate(ks):
-                    bank = "p%d" % (5 + c % 2)
-                    k0, k1 = b0 + kk[0] * nc, b0 + (kk[-1] + 1) * nc
-                    outs = [(ap(bank, i * nc, i * nc + nc), k) for i, k in enumerate(kk)]
-                    xd, yd = [], []
-                    for (o, k) in outs:
-                        one = [None, (o, ap("I"), ap("xb", xo + b0 + k, xo + b1, 16)), (o, ap("In"), Kc("d"))]
-                        xd += one
-                        yd += one + [(o, ap("I"), ap("dl", xo + b0 + k, xo + b1, 16))]
-                    mm(xd[1:])
-                    act(ap("az", k0, k1), ap(bank, 0, len(kk) * nc), F_.Abs)
-                    bank = "p%d" % (5 + (c + 1) % 2)
-                    mm([e and (ap(bank, e[0][2], e[0][3]), e[1], e[2]) for e in yd[1:]])
-                    act(ap("zb", k0, k1), ap(bank, 0, len(kk) * nc), F_.Abs)
-                    mm([(p3, sel("W", k), ap("az", b0 + k * nc, b0 + k * nc + nc)) for k in kk], False, False)
-                    mm([(py, sel("W", k), ap("zb", b0 + k * nc, b0 + k * nc + nc)) for k in kk], False, False)
-                mm([(p3, ap("I4n"), Kc("m01")), (py, ap("I4"), Kc("m01"))], False, True)
-                act(ap("sg2", 2 * j0, 2 * j1), ap("p3", 0, 2 * nc), F_.Sign, bias=col("bs", 3))
-                mm([(ap("p4", 0, nc), ap("Tri"), ap("sg2", 2 * j0, 2 * j0 + nc)), (ap("p4", 0, nc), ap("Tri"), ap("sg2", 2 * j0 + nc, 2 * j1))])
-                act(Kc("lte"), ap("p4", 0, nc), F_.Relu, bias=col("cf", 7), scale=-0.5)
-            else:
-                for si, (s0, s1) in enumerate(subs):
-                    zs = ap("zb", 16 * s0, 16 * s1)
-                    either(zs, ind(Xw, ap("Z16", s0, s1)))
-                mm([(p3, ap("Sh"), Kc("lts"))], True, False)
-                for bi, kk in enumerate(ks):
-                    bank = "p%d" % (5 + (bi + c) % 2)
+                    bank = ZB[zn[0] % len(ZB)]
+                    zn[0] += 1
                     grp = []
                     for i, k in enumerate(kk):
-                        o = ap(bank, i * nc, i * nc + nc)
-                        grp += [None, (o, ap("I"), ap("zb", b0 + k, b1, 16)), (o, ap("In"), Kc("d"))]
+                        o = ap(bank, i * nu, i * nu + nu)
+                        grp += [None, (o, ap("I"), ap("zb", 16 * u0 + k, 16 * u1, 16)), (o, ap("In"), du)]
                     mm(grp[1:])
-                    if bi % 2 == 1 and bi // 2 < cfg["AV"][c]:
-                        mm([e for k in kk for e in ((p3, sel("Wn", k), ap("zb", b0 + k, b1, 16)), (p3, sel("W", k), Kc("d")))], False, False)
-                        ts(ap("az", b0 + kk[0] * nc, b0 + (kk[-1] + 1) * nc), ap(bank, 0, len(kk) * nc), 0.0, A_.max)
-                        mm([(p3, sel("W2", k), ap("az", b0 + k * nc, b0 + k * nc + nc)) for k in kk], False, bi == len(ks) - 1)
-                        continue
-                    act(ap("az", b0 + kk[0] * nc, b0 + (kk[-1] + 1) * nc), ap(bank, 0, len(kk) * nc), F_.Abs)
-                    mm([(p3, sel("W", k), ap("az", b0 + k * nc, b0 + k * nc + nc)) for k in kk], False, bi == len(ks) - 1)
-                act(ap("sg2", 2 * j0, 2 * j0 + nc), p3, F_.Sign, bias=col("bs", 1))
-                mm([(ap("p4", 0, nc), ap("Tri"), ap("sg2", 2 * j0, 2 * j0 + nc))])
-                act(Kc("lte"), ap("p4", 0, nc), F_.Relu, bias=col("cf", 7), scale=-1.0)
-            where[1] = "d"
-            tt(Kc("te"), df, Kc("lte"), A_.mult)
-            tt(Kc("E"), Kc("E"), Kc("te"), A_.add)
-            if late:
-                ef = ap("Ef", 128 * t, 128 * t + nc)
-                send(ef, Kc("E"), t + 2)
-            cp(ind(ap("G", 2 * j0, 2 * j1), ap("cx16", o32 + a0, o32 + a1)), Kc("E"))
-            if late:
-                cp(ind(gf, ap("clf", 16 * t + a0, 16 * t + a1)), ef)
-            elif not last:
-                send(gf, ap("G", 2 * j0, 2 * j1), t + 2)
+                    ops[-1]["key"] = "pz"
+                    az = ap("az", 16 * u0 + kk[0] * nu, 16 * u0 + (kk[-1] + 1) * nu)
+                    w = "W"
+                    if bi >= len(ks) - nv:
+                        mm([(o3, sel("Wn", k), ap("zb", 16 * u0 + k, 16 * u1, 16)) for k in kk], False, False)
+                        relu(az, ap(bank, 0, len(kk) * nu))
+                        w = "W2"
+                    else:
+                        act(az, ap(bank, 0, len(kk) * nu), F_.Abs)
+                    mm([(o3, sel(w, k), ap("az", 16 * u0 + k * nu, 16 * u0 + k * nu + nu)) for k in kk], False, bi == len(ks) - 1)
+            relu(Kc("sg2"), p0, col("bs", 1))
+            if shared:
+                mm(names(p1) + [(p1, ap("T8n"), Kc("sg2")), None, (p0, ap("T8"), Kc("sg2"))])
             else:
-                dma(ap("yl", 2 * j0, 2 * j1), ap("G", 2 * j0, 2 * j1), 1024 * nc)
-            mm([(ap("p4", 0, na), ap("I"), ap("bL", 0, na))] +
-               [(ap("p4", 0, na), sel("W", l), ap("lte", j0 + l, j1, 16)) for l in range(16)])
-            if both:
-                pe = ap("p4", 16, 16 + na)
-                mm([(pe, ap("I"), ap("bL", 0, na))] + [(pe, sel("Wl", l), ap("m01", j0 + l, j1, 16)) for l in range(16)] +
-                   [(pe, sel("W", l), ap("lte", j0 + l, j1, 16)) for l in range(16)])
-            eL = ap("eL", a0, a1)
-            ts(eL, ap("p4", 0, na), -1.0, A_.add)
-            if both:
-                eD = ap("eD", a0, a1)
-                ts(eD, ap("p4", 16, 16 + na), 4095.0, A_.add, 16.0 * nc, A_.min)
-                tt(Kc("vq"), ind(ap("xb", xo + b0, xo + b1), eL), Kc("dm"), A_.add)
-                tt(Kc("q2"), ind(ap("dl", xo + b0, xo + b1 + PAD), eD), Kc("vq"), A_.add)
+                mm([(p0, ap("T8"), Kc("sg2"))])
+                mm([(p1, ap("T8n"), Kc("sg2"))], False, True)
+            where[0] = "e%d%d" % (t, c)
+            Gc = ap("G", 2 * j0, 2 * j1)
+            Go = ind(Gc, ap("cx16", o32 + a0, o32 + a1))
+            En = "Eh" if cfg["EP"][c] else "E"
+            gf = ap("Gf", 512 * t + 2 * j0, 512 * t + 2 * j1)
+            ahead = cfg["EP"][c] and not last
+            if ahead:
+                send(gf, Gc, t + 2)
+                send(ap("clf", 16 * t + a0, 16 * t + a1), ap("cx16", o32 + a0, o32 + a1), t + 2)
+            tt(Kc("em"), p0, Kc(En if t else "Ei"), A_.min)
+            if cfg["ET"][c] == 2 or last:
+                relu(Kc("ea"), p1)
+                tt(Go, Kc("ea"), Kc("em"), A_.add)
+                if not last:
+                    gather(Kc("E"), Go)
             else:
-                tt(Kc("q2"), ind(ap("zb", b0, b1), eL), Kc("dm"), A_.add)
+                tt(Kc(En), p1, Kc("em"), A_.max)
+                if ahead:
+                    ef = ap("Ef", 256 * t + j0, 256 * t + j1)
+                    send(ef, Kc(En), t + 2)
+                cp(Go, Kc(En))
             if last:
-                ts(Kc("q"), Kc("q2"), 0.5, A_.mult, -EVEN / 2, A_.add)
-                dma(ap("yq", j0, j1), Kc("q"), 256 * nc)
-        where[0], where[1] = "x", "a"
-        if not last:
-            ts(ap("q"), ap("q2"), 0.5, A_.mult, -EVEN / 2, A_.add)
-        cxl = ap("cx16", o32 + 16, o32 + 32)
-        tt(ap("xo"), ind(Xw, cxl), ap("dm"), A_.add)
-        ts(ap("x2"), ap("xo"), 0.5, A_.mult, -EVEN / 2, A_.add)
-        cp(ind(ap("X2") if last else Xw, cxl), ap("x2"))
-    dma(ap("yx", 0, 1024), ap("X2", 0, 1024), 262144)
-    dma(ap("yx", 1024, 2048), ap("X2", 1024, 2048), 262144)
+                dma(ap("yl", 2 * j0, 2 * j1), Gc, 1024 * nc)
+            elif ahead:
+                cp(ind(gf, ap("clf", 16 * t + a0, 16 * t + a1)), ef)
+                ops[-1]["key"] = "Gf%d" % c
+            else:
+                send(gf, Gc, t + 2)
+            nought(Kc("lte"), p0)
+            tolist(ap(kb, 0, na), "W", "lte", j0, j1, base)
+            eL = ap("eL", a0, a1)
+            ts(eL, ap(kb, 0, na), -1.0, A_.add)
+            tt(Kc("q2"), ind(ap("zb", b0, b1), eL), Kc("dm"), A_.add)
+            if last:
+                halved(Kc("q"), Kc("q2"))
+                dma(ap("yq", j0, j1), Kc("q"), 256 * nc, "S")
+        where[0] = "x%d" % t
+        parts = pieces(0, C, cfg["SR"])
+        for (j0, j1) in parts:
+            tt(ap("xo", j0, j1), ind(Xw, ap("cx16", o32 + 16 + j0 // 16, o32 + 16 + j1 // 16)), ap("dm", j0, j1), A_.add)
+            halved(ap("x2", j0, j1), ap("xo", j0, j1))
+        for (j0, j1) in parts:
+            cp(ind(Xn, ap("cx16", o32 + 16 + j0 // 16, o32 + 16 + j1 // 16)), ap("x2", j0, j1))
+    dma(ap("yx", 0, 1024), ap("X1", 0, 1024), 262144)
+    dma(ap("yx", 1024, 2048), ap("X1", 1024, 2048), 262144)
     return ops
 
 
@@ -633,78 +648,30 @@ def variant(o, e):
     return o if o["eng"] == e else o["alt"]
 
 
-def prepare(ops, pred, K):
-    n = len(ops)
-    succ = [[] for _ in range(n)]
-    left = [0] * n
-    for i in range(n):
-        for j in sorted(set(pred[i]) | set(ops[i].get("aft", []))):
-            kind = 0 if ops[i]["kind"] == "arr" else 1 if (ops[j]["eng"] == "P" and ops[i]["eng"] == "P") or j not in pred[i] else 2
-            succ[j].append((i, kind))
-            left[i] += 1
-    prio = [0.0] * n
-    for i in range(n - 1, -1, -1):
-        gap = (0.0, ops[i]["occ"], ops[i]["lat"] + K["wake"])
-        prio[i] = max([gap[k] + prio[s] for (s, k) in succ[i]] + [ops[i]["lat"]])
-    return succ, left, prio
+def classes(ops):
+    seen, out = {}, []
+    for o in ops:
+        g, key = o["grp"], o["key"]
+        if o["kind"] == "send" or key[:2] == "cx":
+            key = key[:2]
+        base, t = key + g[0] + g[2:] + ("" if o["kind"] == "c" else o["kind"][0]), int(g[1:2] or 0)
+        k = seen.get((base, t), 0)
+        seen[(base, t)] = k + 1
+        out.append((base + ("." + str(k) if k else ""), t))
+    return out
 
 
-def schedule(ops, prep, K, bias):
-    n = len(ops)
-    succ, left = prep[0], list(prep[1])
-    prio = [prep[2][i] + bias.get(ops[i].get("key"), 0) + bias.get(ops[i].get("grp"), 0) for i in range(n)]
-    other = [prio[i] + bias.get("alt", -2000) + bias.get("~" + ops[i]["key"], 0) if "alt" in ops[i] else 0.0 for i in range(n)]
-    ready = [0.0] * n
-    start = [0.0] * n
-    free = {e: 0.0 for e in "VSPGY"}
+def timed(ops, pred, table, period):
+    tau = {w.split("@")[0].rstrip("*"): (float(w.split("@")[1]), "*" in w) for w in table.split()}
+    key, names = [], classes(ops)
+    for i, (name, t) in enumerate(names):
+        before = [key[j] + 0.00001 for j in pred[i]]
+        key.append(max(before + ([tau[name][0] + period * t] if ops[i]["eng"] else [])))
     order = {e: [] for e in "VSPGY"}
-    pool = {e: [] for e in "VSPGY"}
-    end = [0.0]
-
-    def release(i, o):
-        gap = (0.0, o["occ"], o["lat"] + K["wake"])
-        end[0] = max(end[0], start[i] + o["lat"])
-        for (s, k) in succ[i]:
-            if start[i] + gap[k] > ready[s]:
-                ready[s] = start[i] + gap[k]
-            left[s] -= 1
-            if left[s] == 0:
-                if ops[s]["eng"] is None:
-                    start[s] = ready[s]
-                    release(s, ops[s])
-                else:
-                    pool[ops[s]["eng"]].append(s)
-                    if "alt" in ops[s]:
-                        pool["V"].append(s)
-    for i in range(n):
-        if left[i] == 0:
-            pool[ops[i]["eng"]].append(i)
-    look = bias.get("look", 40)
-    while True:
-        best = None
-        for e in "SVPGY":
-            if pool[e]:
-                tm = max(free[e], min([ready[i] for i in pool[e]]))
-                if best is None or tm < best[0]:
-                    best = (tm, e)
-        if best is None:
-            break
-        tm, e = best
-        i, top = -1, None
-        for c in pool[e]:
-            if ready[c] <= tm + look:
-                p = prio[c] if ops[c]["eng"] == e else other[c]
-                if top is None or p > top:
-                    i, top = c, p
-        pool[e].remove(i)
-        if "alt" in ops[i]:
-            pool["S" if e == "V" else "V"].remove(i)
-        o = variant(ops[i], e)
-        start[i] = max(tm, ready[i])
-        free[e] = start[i] + o["occ"]
-        order[e].append(i)
-        release(i, o)
-    return order, start, end[0]
+    for i in sorted(range(len(ops)), key=lambda i: key[i]):
+        if ops[i]["eng"]:
+            order["V" if tau[names[i][0]][1] else ops[i]["eng"]].append(i)
+    return order
 
 
 PLAN = []
@@ -717,7 +684,7 @@ def rank_program(g, core, T, topo):
     if not PLAN:
         ops = build(CFG, COST)
         pred = depend(ops)
-        PLAN.append((ops, pred, schedule(ops, prepare(ops, pred, COST), COST, BIAS)[0]))
+        PLAN.append((ops, pred, timed(ops, pred, TIMES, PERIOD)))
     ops, pred, order = PLAN[0]
     queue = {"V": g.vector, "S": g.scalar, "P": g.tensor, "G": g, "Y": g.sync}
 

import numpy as np
from concourse.bass import DstId, RemoteDMATransfer
from concourse.mybir import dt, AluOpType, AxisListType, ActivationFunctionType

N, STEPS, C = 8, 4, 256
F16, BF, F32, I32, U16 = "float16", "bfloat16", "float32", "int32", "uint16"
CFG = {
    "CH": [128, 128],
    "NG": [0, 1, 2],
    "SX": [[32, 48, 48], [48, 48, 32]],
    "SZ": [[64, 64], [32, 32, 32, 32]],
    "U1": [64, 64],
    "U2": [64, 64],
    "SC": [64, 64],
    "AB": [1, 1],
    "LS": [0, 0],
    "ET": [1, 1],
    "CC": [1, 1],
    "EP": [0, 1],
    "SR": 128,
    "D3": 1,
    "AV": [0, 0],
    "PS": [0, 0],
    "MP": [0, 0],
    "D2": [0, 0],
    "ONV": ["WD0_0", "zb3584", "zb2560", "q0", "q128", "x2_0"],
    "DG": 520,
}
BIAS = {}
PERIOD = 2900
TIMES = """
ci0i@-8003 Xr0i@-7922 Dw0i@-7751 Dw1560i@-7549 wc0id@-7094 ci2i@-7023 ai0i*@-6781 ci1i@-6568 pm2064i@-6548 Dw1040i@-6508 cf0i@-6467 W0i@-6397 cf8i*@-5750 bI16i@-5689 I0i@-5507 nd0i@-5477 Dw520i@-5467 Ww0i@-5265 pm0i@-5245 K16_0i@-5204 jk128i@-5053 Ds0id@-4790 Gi0id@-4618 X16_0i@-4396 Dlis@-4386 Gi256id@-4305 Gais@-4214 Gais.1@-4164 Lr0i@-3618 q0id@-3517 Tv0i@-3052 bL0i@-2830 cf11i@-2769 Tv1024i@-2557 In16_0i@-2274 WD0_0i@-2213 bI0i@-2143 I4_0i*@-1769 W15_0i@-1668 Tc0i@-1526 cf10i*@-1516 jk0i@-1355 Tc1024i@-960 I16_0i@-627 Dw0id@-516 u0_0n@-506 X0_0id@-496 pu0n@-475 u0n@-455 ub0n@-445 cf7i*@-425 Wh0i@-405 t3_0n@-395 Ei0id@-384 t2_0n@-354 t1_0n@-324 bI8i@-314 ub16n@-304 cL0n@-294 thi0id@-273 nI0n@-263 Dg0n@-243 q0b0@-233 Ih16_0i*@-213 n16_0n@-203 Dg128n*@-182 q128b1@-172 WD1_0i@-142 BO0i@-132 u8n@-122 G0i@-112 t1_8n@-102 cf9i@-91 u0_8n@-81 PB0n@-51 Dw0nd@-41 pc0n@-31 pu1n@-21 t2_8n@-11 Sh0i@0 cf17i@10 uc0n@20 t3_8n@30 T8_0i@40 BOn2_0i@60 E8_0i@80 nI8n@90 cxn@101 xb0a0@121 Dg2_128n*@141 thf0i@161 BOn0i*@171 po0n@202 pc1n@212 p3_0i@222 km0i@232 Dg2_0n@242 n16_8n@252 T8n0i*@272 Cm0i@282 xb512a0@303 dl512a0@353 po1n@363 cL16n@373 km15i@383 nr0d@394 xb1280a0@404 bs0i@414 nh0d@424 cL8n@434 PB256n@444 p4_0d@454 bs2i*@464 BO2_0i*@474 xb2816a1@485 xb2048a1@495 PB128n@505 dl0a0@515 rl512a0@525 p4_0d.1@545 eq0d@565 rl0a0@575 cL24n@586 dl1280a0@606 rl1280a0@616 nd0d@636 PB384n@646 pm1a0@656 Vc0d@666 p0_0b0@677 dl2816a1@707 p0_64b0@717 p0_0b0.1@727 dl2048a1@737 Dw0d@767 xb3584a1@788 bs1i*@798 m01_0b0@808 dl3584a1@818 Dx1024i@828 sg0b0@838 Dw0d.1@848 sL0b0@858 pm1025a0@868 rl2816a1@879 Dw0d.2@889 PBf0n@899 lts0b0@909 rl2048a1@919 rl3584a1@939 Dw0d.3@959 p0_0b0.2@970 bs3i@980 Dw0d.4@990 mq0b0@1000 pm2065a1@1030 ab0b0@1040 ab128b0@1050 rb128b0@1060 rb0b0@1071 Dw0d.5@1081 Dw0d.11@1091 d0b0@1101 Dw0d.6@1111 lts128b1@1121 dm0b0@1141 p1_64b1@1162 p1_0b1@1172 Dw0d.15@1192 pm3089a1@1202 p1_0b1.1@1212 sg128b1@1222 p0_0b0.3@1242 In0i@1252 p0_128b0@1263 p1_0b1.2@1273 zb2048c1*@1283 Dw0d.7@1293 ab256b1@1303 d128b1@1313 tz0b0@1323 sL8b1@1333 Dw0d.8@1343 mq128b1@1354 zb0c0@1394 p0_0b0.4@1424 Z16_0b0@1434 PBf256n@1444 ab384b1@1455 rb256b1@1465 rb384b1@1475 Dw0d.9@1485 p1_128b1@1505 zb2560c1*@1515 xo0x@1525 p1_0b1.3@1535 m01_128b1@1556 p3_0c0@1566 Dw0d.10@1576 p0_0c0@1596 Dw0d.12@1616 Dw0d.13@1626 zb1024c0@1647 pzc0@1657 tz128b1@1667 p1_0b1.4@1687 az64c0@1697 X1_0x.1@1707 zb3584c1*@1717 Dw0d.14@1727 zb3072c1*@1737 pzc0.1@1748 x2_0x@1758 az576c0@1768 p1_0c1@1778 Z16_128b1@1798 pzc0.2@1808 p0_0c0.1@1818 pzc0.3@1828 pzc1@1839 p0_0c0.2@1849 xo128x@1859 az1088c0@1869 p0_64c0@1879 az1600c0@1889 p0_64c0.2@1899 p0_64c0.1@1909 Dx0i@1929 em0e0@1950 dm128b1@1960 pzc1.1@1970 sg2_0c0@1980 Gfe1s@1990 pzc1.3@2000 p0_0c0.3@2010 p3_0c0.1@2020 p0_0e0@2031 pzc1.2@2041 X0_0x@2051 az2112c1@2061 p1_0c1.1@2071 lte0e0@2081 az2624c1@2091 az3136c1@2101 cle1s@2111 az3648c1@2121 p1_0c1.2@2142 ea0e0*@2162 X1_0nd@2172 x2_128x*@2202 E0e0@2212 X1_0x@2222 p1_64c1@2243 p1_64c1.1@2253 p1_64c1.2@2263 sg2_128c1@2293 Ds0dd@2313 q2_0e0@2324 G0e0@2334 eL0e0@2344 q0e0@2354 p3_0c1.1@2364 X0_0x.1@2414 p1_0c1.3@2435 em128e1@2465 ac4b0@2485 p1_0e1@2526 p4_500b1@2536 p3_0c1@2556 lte128e1@2566 Eh128e1@2617 yx1024xd@2647 ea128e1*@2677 G256e1@2708 eL8e1@2738 q2_128e1@2829 Dlds@2839 yx0xd@3051 Dx0dd@3081 Gfe0s@3091 Efe1s@3162 Gf1e1@3213 yl0e0d@3829 yl256e1d@3920 yq0e0d@4264 q128e1*@4688 yq128e1d@5274
"""
EVEN = 2560.0
BIG = 8192.0


def sb(cols, dtype):
    return ("sbuf", [128, cols], dtype)


SCRATCH = {
    "X0": sb(2048, BF), "X1": sb(2048, BF), "G": sb(512, F32), "Gi": sb(512, I32), "Gf": sb(1536, F32), "Ga": sb(512, I32),
    "Dw": sb(2064, I32), "Dx": sb(2048, I32), "Ds": sb(128, I32), "Dl": sb(512, I32), "Tv": sb(2048, F32), "Tc": sb(2048, F32),
    "xb": sb(4096, BF), "dl": sb(4096, BF), "rl": sb(4096, BF), "pm": sb(4096 + 128, BF), "zb": sb(4096, BF), "az": sb(4096, BF),
    "q": sb(256, BF), "q2": sb(256, F16), "Ei": sb(256, I32), "E": sb(256, F32), "ea": sb(256, F32), "em": sb(256, F32),
    "wc": sb(16, BF), "K16": sb(16, F32), "thi": sb(4, I32), "thf": sb(4, F32), "ci": sb(8, I32), "cf": sb(20, F32), "bs": sb(4, F32),
    "Xr": sb(144, F32), "X16": sb(128, F32), "Lr": sb(256, BF), "ai": sb(16, F32), "bI": sb(32, I32), "bL": sb(16, BF),
    "W": sb(144, BF), "W2": sb(144, BF), "Wn": sb(144, BF), "Ww": sb(144, BF), "Wh": sb(144, F16),
    "WD0": sb(144, F16), "WD1": sb(144, F16), "I": sb(128, BF), "In": sb(128, BF), "I16": sb(128, F16), "In16": sb(128, F16),
    "Ih16": sb(128, F16), "Ihn": sb(128, F16), "I4": sb(128, BF), "Sh": sb(128, BF), "BO": sb(128, BF), "BO2": sb(128, BF),
    "BOn": sb(128, BF), "BOn2": sb(128, BF), "T8": sb(128, BF), "T8n": sb(128, BF), "W15": sb(128, F32), "E8": sb(128, F32),
    "Cm": sb(256, BF), "BK": sb(512, BF), "km": sb(2048, BF), "jk": sb(256, BF),
    "u0": sb(16, I32), "u": sb(16, I32), "t1": sb(16, I32), "t2": sb(16, I32), "t3": sb(16, I32), "nI": sb(16, I32),
    "ub": sb(32, I32), "uc": sb(32, I32), "n16": sb(16, U16), "cx16": sb(64, U16), "nh": sb(16, F16),
    "cL": sb(32, U16), "nd": sb(32, U16), "sL": sb(16, U16), "eL": sb(16, U16),
    "Dg": sb(256, F16), "Dg2": sb(256, F16), "nr": sb(256, F32), "Vc": sb(256, F32), "eq": sb(256, BF),
    "PB": sb(512, U16), "PBf": sb(512, F16), "Mg": sb(256, BF), "Z16": sb(256, U16), "tz": sb(256, F16),
    "sg": sb(256, BF), "lts": sb(256, BF), "sg2": sb(256, BF), "lte": sb(256, BF), "mq": sb(256, BF), "d": sb(256, BF),
    "dm": sb(256, F32), "ab": sb(512, BF), "rb": sb(512, BF), "m01": sb(256, BF), "ac": sb(8, F32),
    "Eh": sb(256, F16), "Ef": sb(768, F16), "clf": sb(48, U16), "xo": sb(256, F16), "x2": sb(256, BF),
}
for _b in range(8):
    SCRATCH["p%d" % _b] = ("psum", [128, 512], F32)
SEMAPHORES = ["V", "S", "P", "G"] + ["m%d" % i for i in range(70)] + ["a%d" % i for i in range(30)]
IO = {"xr": 2, "lg": 4, "dr": 4, "qd": 2, "e0": 4, "wt": 2, "th": 4, "yl": 4, "yx": 2, "yq": 2}
SIZE = {F32: 4, I32: 4, BF: 2, F16: 2, U16: 2}
COST = {"cyc": 0.92, "pe": 0.5, "fix": 60.0, "wake": 80.0, "gat": 1.56, "sca": 3.8, "tt2": 1.0, "dma": 1700.0, "rem": 2200.0,
        "issue": 600.0, "lbw": 150.0, "rbw": 50.0, "dq": 100.0}
A_ = AluOpType
F_ = ActivationFunctionType


def ap(name, c0=0, c1=None, step=1, rows=None):
    if c1 is None:
        c1 = SCRATCH[name][1][1] if name in SCRATCH else -1
    return ("ap", name, c0, c1, step, rows)


def ind(win, off):
    return ("ind", win, off)


def is_ap(a):
    return isinstance(a, tuple) and len(a) > 0 and a[0] in ("ap", "ind")


def count(a):
    if a[0] == "ind":
        return 16 * count(a[2])
    return (a[3] - a[2] + a[4] - 1) // a[4]


def width(a):
    n = a[1][1] if a[0] == "ind" else a[1]
    return SIZE[SCRATCH[n][2]] if n in SCRATCH else IO[n]


def in_psum(a):
    return a[0] == "ap" and a[1] in SCRATCH and SCRATCH[a[1]][0] == "psum"


def regions(a):
    if a[1] not in SCRATCH:
        return []
    if in_psum(a):
        return [(a[1], 0, 512)]
    if a[1] == "Dw":
        return [("Dwr%d" % r, a[2], a[3]) for r in (0, 1) if a[5] is None or a[5][0] == r]
    return [(a[1], a[2], a[3])]


def real(T, a):
    if a[0] == "ind":
        return real(T, a[1]).indirect(real(T, a[2]))
    t = T[a[1]]
    if a[3] < 0:
        return t[:]
    r = slice(None) if a[5] is None else slice(*a[5])
    return t[r, a[2]:a[3]] if a[4] == 1 else t[r, a[2]:a[3]:a[4]]


def pieces(lo, hi, size):
    return [(s, min(s + size, hi)) for s in range(lo, hi, size)]


def cuts(lo, sizes):
    return [(lo + sum(sizes[:i]), lo + sum(sizes[:i + 1])) for i in range(len(sizes))]


def build(cfg, K):
    ops = []
    where = ["i"]

    def add(eng, calls, occ, lat, kind="c", extra=None):
        rd, wr = [], []
        for (m, args, kw) in calls:
            for i, a in enumerate(list(args) + list(kw.values())):
                if not is_ap(a):
                    continue
                out = i == 0 or (i >= len(args) and a is kw.get("accum_out"))
                if a[0] == "ind":
                    rd.extend(regions(a[2]))
                    a = a[1]
                (wr if out or in_psum(a) else rd).extend(regions(a))
        a = extra[0] if kind == "send" else calls[0][1][0]
        a = a[1] if a[0] == "ind" else a
        ops.append({"eng": eng, "calls": calls, "occ": occ, "lat": lat, "kind": kind, "rd": rd, "wr": wr, "x": extra,
                    "key": "%s_%d" % (a[1], a[2]) if a[1][-1] in "0123456789" else "%s%d" % (a[1], a[2]), "grp": where[0]})

    def ecost(m, args):
        aps = [a for a in args if is_ap(a) and (a[0] == "ind" or count(a) > 1 or a is args[0])]
        n = max(count(a) if a[0] == "ind" or a is args[0] else 0 for a in aps)
        if aps[0][0] == "ind":
            c = n * K["sca"]
        elif any(a[0] == "ind" for a in aps):
            c = n * K["gat"]
        else:
            two = all(width(a) == 2 for a in aps)
            if m == "tensor_tensor":
                c = n * (1.0 if any(in_psum(a) for a in aps[1:]) else (K["tt2"] if two else 2.0))
            elif m == "activation":
                c = n
            else:
                c = n * (0.5 if two else 1.0)
            c = max(c, K.get("min", 0))
        return (K.get("sfix", K["fix"]) if m == "activation" else K["fix"]) + c * K["cyc"]

    def V(m, *args):
        c = ecost(m, args)
        add("V", [(m, args, {})], c, c)

    def tt(o, a, b, op):
        V("tensor_tensor", o, a, b, op)

    def tsargs(o, a, s1, op0, s2=None, op1=None):
        return (o, a, s1, None, op0) if op1 is None else (o, a, s1, s2, op0, op1)

    def ts(*args):
        V("tensor_scalar", *tsargs(*args))

    def cp(o, a):
        V("tensor_copy", o, a)

    def act(o, a, f, **kw):
        c = ecost("activation", (o, a))
        add("S", [("activation", (o, a, f), kw)], c, c)

    def alt(m, *args):
        c = ecost(m, args)
        ops[-1]["alt"] = {"eng": "V", "calls": [(m, args, {})], "occ": c, "lat": c}

    def gather(o, a):
        act(o, a, F_.Copy)
        alt("tensor_copy", o, a)

    def relu(o, a, bias=None):
        if bias is None:
            act(o, a, F_.Relu)
            alt("tensor_scalar", *tsargs(o, a, 0.0, A_.max))
        else:
            act(o, a, F_.Relu, bias=bias)
            alt("tensor_scalar", *tsargs(o, a, bias, A_.add, 0.0, A_.max))

    def nought(o, a):
        act(o, a, F_.Relu, scale=-1.0, bias=1.0)
        alt("tensor_scalar", *tsargs(o, a, 0.5, A_.is_lt))

    def affine(o, a, f, b=0.0):
        act(o, a, F_.Identity, scale=f, bias=b)
        alt("tensor_scalar", *tsargs(o, a, f, A_.mult, b, A_.add))

    def halved(o, a):
        affine(o, a, 0.5, -EVEN / 2)

    def mm(group, start=True, stop=True):
        calls, c = [], 0.0
        for i, e in enumerate(group):
            if e is None:
                continue
            o, l, r = e
            calls.append(("matmul", (o, l, r, start if i == 0 else group[i - 1] is None,
                                     stop if i == len(group) - 1 else group[i + 1] is None), {}))
            c += max(min(64, count(l)), count(r)) * (4 if width(r) == 4 else 1) * K["pe"] + K.get("pfix", 0)
        add("P", calls, c, c + K["fix"])

    def iota(o, pat, base, cm):
        kw = {} if SCRATCH[o[1]][2] == I32 else {"allow_small_or_imprecise_dtypes": True}
        c = 130 + 2 * count(o) * K["cyc"]
        add("G", [("iota", (o, pat, base, cm), kw)], c, c)

    def dma(o, i, nbytes, eng="Y"):
        add(eng, [("dma_start", (o, i), {})], K["dq"], K["dma"] + nbytes / K["lbw"], "dma")
        ops[-1]["flow"] = nbytes / K["lbw"]

    def send(o, i, back):
        nb = 128 * count(i) * width(i)
        add("G", [("remote", (None, i), {})], K["issue"], K["issue"] + 1000 + nb / K["rbw"], "send", (o, back))
        ops[-1]["flow"] = nb / K["rbw"]
        ops.append({"eng": None, "calls": [], "occ": 0.0, "lat": K["rem"] + nb / K["rbw"], "kind": "arr", "rd": [],
                    "wr": regions(o), "x": len(ops) - 1, "key": "arr", "grp": where[0]})

    def sel(name, k):
        return ap(name, 15 - k, 143 - k)

    def col(name, j):
        return ap(name, j, j + 1)

    def tolist(o, w, name, j0, j1, first=()):
        mm(list(first) + [(o, sel(w, l), ap(name, j0 + l, j1, 16)) for l in range(16)])

    CH = cfg["CH"]
    nch = len(CH)
    J = [sum(CH[:i]) for i in range(nch + 1)]
    CB = ["p0", "p1", "p2", "p3"][:nch]
    CC = ["p3" if cfg["CC"][c] else CB[c] for c in range(nch)]
    ZB, zn = ["p5", "p6"] + [b for b in ("p2", "p3") if b not in CB + CC], [0]
    book0, book1 = ap("Dw", 0, 2048, 1, (0, 128, 16)), ap("Dw", 0, 2048, 1, (1, 128, 16))
    dma(ap("q"), ap("qd"), 65536)
    dma(col("wc", 0), ap("wt"), 4096, "S")
    dma(ap("Ds"), ap("dr"), 65536)
    dma(ap("Gi", 0, 256), ap("lg", 0, 256), 131072, "S")
    dma(ap("Gi", 256, 512), ap("lg", 256, 512), 131072, "S")
    dma(ap("thi", 0, 2, 1, (0, 8)), ap("th"), 1024, "S")
    iota(col("ci", 0), [[0, 1]], 0, 1)
    iota(ap("Xr"), [[1, 144]], 0, 0)
    dg = cfg["DG"]
    if dg:
        iota(ap("Dw", 0, dg), [[0, dg]], 0, 0)
    for (m0, m1) in pieces(dg, 2064, 520):
        V("memset", ap("Dw", m0, m1), 0)
    dma(book0, ap("dr"), 65536)
    dma(ap("X0"), ap("xr"), 524288)
    dma(ap("Ei"), ap("e0"), 131072, "S")
    ts(col("ci", 1), col("ci", 0), 112, A_.bitwise_and)
    ts(col("ci", 2), col("ci", 0), 15, A_.bitwise_and)
    cp(ap("cf", 0, 3), ap("ci", 0, 3))
    pc, gc, kc = col("cf", 0), col("cf", 1), col("cf", 2)
    ts(ap("W"), ap("Xr"), gc, A_.subtract, 15.0, A_.is_equal)
    ts(ap("Ww"), ap("W"), col("wc", 0), A_.mult)
    send(ap("Dl", 0, 128), ap("Ds"), 1)
    send(ap("Ga", 0, 256), ap("Gi", 0, 256), 1)
    send(ap("Ga", 256, 512), ap("Gi", 256, 512), 1)
    ts(ap("K16"), ap("Xr", 0, 16), kc, A_.is_equal)
    k0, k1, k15 = col("K16", 0), col("K16", 1), col("K16", 15)
    affine(col("cf", 7), k15, -1.0, 1.0)
    affine(col("cf", 8), kc, 1.0, 2048.0)
    affine(col("cf", 9), pc, 16.0)
    affine(col("cf", 10), k0, -BIG)
    affine(ap("WD0"), ap("W"), k0)
    affine(ap("WD1"), ap("W"), k1)
    affine(ap("Wh"), ap("Ww"), 0.5)
    if not all(cfg["AB"]) or any(cfg["AV"]):
        affine(ap("W2"), ap("W"), 2.0)
        affine(ap("Wn"), ap("W"), -1.0)
    x128 = ap("Xr", 0, 128)
    ts(ap("I"), x128, pc, A_.is_equal)
    iota(ap("X16"), [[16, 8], [0, 16]], 0, 0)
    ts(ap("BO"), ap("X16"), gc, A_.is_equal)
    for (o, s, f) in (("In", "I", -1.0), ("I4", "I", 4096.0), ("BO2", "BO", 2.0), ("BOn", "BO", -1.0), ("BOn2", "BO", -2.0),
                      ("I16", "I", 1.0), ("In16", "I", -1.0), ("Ih16", "I", 0.5)) + ((("Ihn", "I", -0.5),) if any(cfg["MP"]) else ()):
        affine(ap(o), ap(s), f)
    ts(ap("jk", 0, 128), x128, pc, A_.is_ge, BIG, A_.mult)
    tt(ap("T8"), ap("jk", 0, 128), ap("BO"), A_.mult)
    affine(ap("T8n"), ap("T8"), -1.0)
    ts(ap("jk", 128, 256), x128, pc, A_.subtract, 1.0, A_.is_equal)
    affine(col("cf", 17), k15, BIG, -BIG)
    affine(ap("Sh"), ap("jk", 128, 256), col("cf", 17))
    affine(col("cf", 11), k15, 16.0)
    affine(ap("W15"), x128, 0.0, col("cf", 11))
    ts(ap("E8"), ap("X16"), col("cf", 9), A_.is_equal)
    cp(ap("thf", 0, 2, 1, (0, 8)), ap("thi", 0, 2, 1, (0, 8)))
    mm([(ap("p3", 0, 2), ap("E8", 0, 128, 1, (0, 8)), ap("thf", 0, 2, 1, (0, 8))), None, (ap("p3", 2, 3), ap("BO"), col("wc", 0))])
    affine(col("bs", 2), ap("p3", 0, 1), -1.0)
    affine(col("bs", 1), ap("p3", 1, 2), -1.0, col("cf", 10))
    affine(col("bs", 3), ap("p3", 2, 3), -EVEN / 2)
    affine(col("bs", 0), col("bs", 2), col("cf", 7), k15)
    for m in (0, 1024):
        iota(ap("Tv", m, m + 1024), [[1, 1024]], m, 0)
        iota(ap("Tc", m, m + 1024), [[2, 128], [0, 4], [1, 2]], m // 4, 0)
        if cfg["D3"]:
            iota(ap("Dx", m, m + 1024), [[0, 1024]], 0, 0)
    affine(ap("ai"), ap("Xr", 0, 16), 16.0, kc)
    affine(ap("bL"), ap("ai"), 16.0)
    ts(ap("bI", 16, 32), ap("ai"), 8.0, A_.mult)
    for c in range(nch):
        ts(ap("bI", J[c] // 16, J[c + 1] // 16), ap("ai", J[c] // 16, J[c + 1] // 16), 2.0, A_.mult, -2.0 * J[c], A_.add)
    nk = 16 * max(cfg["SC"])
    V("memset", ap("km", 0, nk), 1.0)
    V("memset", ap("km", 15, nk, 16), 0.0)
    PO = [16 * J[c] + 16 * c for c in range(nch)]
    for c in range(nch):
        V("memset", col("pm", PO[c]), 0.0)
    V("memset", ap("nd"), 0)
    cp(ap("G"), ap("Gi"))

    def banks(u):
        per = 512 // u
        return [list(range(k, min(k + per, 16))) for k in range(1, 16, per)]
    BK = {}
    for c in range(nch):
        if cfg["AV"][c]:
            kb0 = banks(cfg["U2"][c])[-cfg["AV"][c]][0]
            if kb0 not in BK:
                BK[kb0] = ap("BK", 128 * len(BK), 128 * len(BK) + 128)
                ts(ap("jk", 0, 128), x128, gc, A_.subtract, float(kb0), A_.is_ge)
                tt(BK[kb0], ap("jk", 0, 128), ap("BO"), A_.mult)
    iota(ap("Lr"), [[0, 16], [1, 16]], 0, 0)
    ts(ap("Cm"), ap("Lr"), kc, A_.is_ge, 4096.0, A_.mult)

    for t in range(STEPS):
        last = t == STEPS - 1
        o32 = 32 * (t % 2)
        Gw = ap("G") if t else ap("Gi")
        Gf = ap("Gf", 512 * t - 512, 512 * t) if t else ap("Ga")
        Xw, Xn = ap("X0"), ap("X1" if last else "X0")
        NG = cfg["NG"]
        groups = [(J[NG[gi]], J[NG[gi + 1]]) for gi in range(len(NG) - 1)]
        where[0] = "n%d" % t
        if last:
            dma(Xn, Xw, 524288)
        late = []
        for gi, (j0, j1) in enumerate(groups):
            a0, a1 = j0 // 16, j1 // 16
            na = a1 - a0

            def L(name):
                return ap(name, a0, a1)
            nb = CB[-1] if gi else "p7"
            if t == 0 and gi == 0:
                a1 = 16
                tolist(ap(nb, 0, 16), "Ww", "q", 0, C)
                cp(L("u0"), ap(nb, 0, 16))
            elif t:
                tolist(ap(nb, 0, na), "Wh", "q2", j0, j1)
                ts(L("u0"), ap(nb, 0, na), col("bs", 3), A_.add)
            ops[-2]["key"] = "pu%d" % gi if t or gi == 0 else ops[-2]["key"]
            if t or gi == 0:
                ts(L("u"), L("u0"), 2047, A_.bitwise_and)
                tt(L("t2"), L("u"), L("u"), A_.mult)
                if t:
                    ts(L("t1"), L("u"), 1184.0, A_.mult, col("p4", 500), A_.add)
                else:
                    ts(L("t1"), L("u"), 1184.0, A_.mult)
                tt(L("t3"), L("t1"), L("t2"), A_.add)
                ts(L("nI"), L("t3"), 5, A_.arith_shift_right, 2047, A_.bitwise_and)
                cp(L("n16"), L("nI"))
            a1 = j1 // 16
            gather(ap("Dg", j0, j1), ind(ap("Dw", 0, 2048), L("n16")))
            tolist(ap(nb, 0, na), "WD0", "Dg", j0, j1)
            ops[-1]["key"] = "pc%d" % gi
            cp(ap("cL", 2 * a0, 2 * a0 + na), ap(nb, 0, na))
            if t == 0 or cfg["D2"][gi] or cfg["D3"]:
                late.append(gi)
            else:
                ob = "p7" if gi else CB[0]
                tolist(ap(ob, 0, na), "WD1", "Dg", j0, j1)
                ops[-1]["key"] = "po%d" % gi
                cp(ap("cL", 2 * a0 + na, 2 * a1), ap(ob, 0, na))
            if (t == 0 and gi == len(groups) - 1) or (t and gi == 0 and cfg["D2"][0]):
                dma(book1, ap("Dl", 128 * t, 128 * t + 128), 65536)
        for gi in late:
            j0, j1 = groups[gi]
            a0, a1 = j0 // 16, j1 // 16
            gather(ap("Dg2", j0, j1), ind(ap("Dx" if cfg["D3"] and t else "Dw", 0, 2048), ap("n16", a0, a1)))
            ob = "p7" if gi else CB[0]
            tolist(ap(ob, 0, a1 - a0), "WD1", "Dg2", j0, j1)
            ops[-1]["key"] = "po%d" % gi
            cp(ap("cL", a0 + a1, 2 * a1), ap(ob, 0, a1 - a0))
        Pn, Bn = {}, {}
        for gi, (j0, j1) in enumerate(groups):
            a0, a1 = j0 // 16, j1 // 16
            both = ((2 * j0, j0 + j1, ind(Gw, ap("cL", 2 * a0, a0 + a1))), (j0 + j1, 2 * j1, ind(Gf, ap("cL", a0 + a1, 2 * a1))))
            if cfg["PS"][gi]:
                for (c0, c1, src) in both:
                    gather(ap("PBf", c0, c1), src)
                    cp(ap("PB", c0, c1), ap("PBf", c0, c1))
            else:
                for (c0, c1, src) in both:
                    cp(ap("PB", c0, c1), src)
                cp(ap("PBf", 2 * j0, 2 * j1), ap("PB", 2 * j0, 2 * j1))
            for c in range(NG[gi], NG[gi + 1]):
                Pn[c], Bn[c] = j0, j1
        ts(ap("ub", 0, 16), ap("u0"), 1, A_.bitwise_and)
        ts(ap("ub", 16, 32), ap("u0"), 7, A_.bitwise_and)
        tt(ap("uc"), ap("ub"), ap("bI"), A_.add)
        cp(ap("cx16", o32, o32 + 32), ap("uc"))
        cxl = ap("cx16", o32 + 16, o32 + 32)
        where[0] = "d%d" % t
        if not last:
            cp(ap("nh"), ap("nI"))
            gather(ap("nr"), ind(ap("Tv"), ap("n16")))
            gather(ap("Vc"), ind(ap("Tc"), cxl))
            mm([(ap("p4", 0, 256), ap("I"), ap("Cm"))] + [(ap("p4", l, 256, 16), ap("I16"), ap("nh")) for l in range(16)])
            tt(ap("eq"), ap("nr"), ap("p4", 0, 256), A_.is_equal)
            mm([(ap("p4", 0, 16), ap("I16"), ap("nh"))] + [(ap("p4", 0, 16), ap("I4"), ap("eq", l, 256, 16)) for l in range(15)])
            ts(ap("nd", 0, 32, 2), ap("p4", 0, 16), col("cf", 8), A_.min)
            for a in range(15, -1, -1):
                cp(ind(ap("Dw"), ap("nd", 2 * a, 2 * a + 1)), ap("Vc", 16 * a, 16 * a + 16))
            dma(ap("Ds"), book0, 65536)
            send(ap("Dl", 128 * t + 128, 128 * t + 256), ap("Ds"), t + 2)
            if cfg["D3"]:
                dma(ap("Dx", 0, 2048, 1, (1, 128, 16)), ap("Dl", 128 * t + 128, 128 * t + 256), 65536)
            elif not cfg["D2"][0]:
                dma(book1, ap("Dl", 128 * t + 128, 128 * t + 256), 65536)
        for c in range(nch):
            j0, j1 = J[c], J[c + 1]
            where[0] = "a%d%d" % (t, c)
            for (s0, s1) in cuts(j0, cfg["SX"][c]):
                xs_, dl_, rl_ = [ap(n, 16 * s0, 16 * s1) for n in ("xb", "dl", "rl")]
                gather(xs_, ind(Xw, ap("PB", Pn[c] + s0, Pn[c] + s1)))
                tt(dl_, ind(Xw, ap("PB", Bn[c] + s0, Bn[c] + s1)), xs_, A_.subtract)
                if cfg["AB"][c]:
                    act(rl_, dl_, F_.Abs)
                else:
                    relu(rl_, dl_)
            for (s0, s1) in pieces(j0, j1, cfg["SC"][c]):
                o = PO[c] + 16 * (s0 - j0) + 1
                V("tensor_tensor_scan", ap("pm", o, o + 16 * (s1 - s0)), ap("xb", 16 * s0, 16 * s1), ap("km", 0, 16 * (s1 - s0)),
                  0.0, A_.max, A_.mult)
        for c in range(nch):
            j0, j1, nc = J[c], J[c + 1], CH[c]
            a0, a1, na = j0 // 16, j1 // 16, CH[c] // 16
            b0, b1 = 16 * j0, 16 * j1
            where[0] = "b%d%d" % (t, c)

            def Kc(name):
                return ap(name, j0, j1)
            P16, B16 = ap("PBf", Pn[c] + j0, Pn[c] + j1), ap("PBf", Bn[c] + j0, Bn[c] + j1)
            kb = CB[c]
            p0, pn = ap(kb, 0, nc), ap(kb, nc, 2 * nc)
            for (u0, u1) in pieces(j0, j1, cfg["U1"][c]):
                o = ap(kb, u0 - j0, u1 - j0)
                if cfg["AB"][c]:
                    mm([(o, sel("W", k), ap("rl", 16 * u0 + k, 16 * u1, 16)) for k in range(15)])
                else:
                    mm([(o, sel("Wn", k), ap("dl", 16 * u0 + k, 16 * u1, 16)) for k in range(15)], True, False)
                    mm([(o, sel("W2", k), ap("rl", 16 * u0 + k, 16 * u1, 16)) for k in range(15)], False, True)
            relu(Kc("sg"), p0, col("bs", 0))
            mm([(p0, ap("T8"), Kc("sg"))])
            nought(Kc("lts"), p0)
            base = [(ap(kb, 0, na), ap("I"), ap("bL", 0, na))]
            tolist(ap(kb, 0, na), "W", "lts", j0, j1, base)
            sL = ap("sL", a0, a1)
            cp(sL, ap(kb, 0, na))
            Mi = ind(ap("pm", PO[c], PO[c] + 16 * nc), sL)
            if cfg["MP"][c]:
                gather(Kc("Mg"), Mi)
                mm([(p0, ap("Ihn"), Kc("q2")) if t else (p0, ap("In"), Kc("q")), (p0, ap("I"), Kc("Mg"))])
                act(Kc("d"), p0, F_.Abs, bias=EVEN / 2 if t else 0.0)
            else:
                if t:
                    halved(Kc("q"), Kc("q2"))
                tt(Kc("mq"), Mi, Kc("q"), A_.subtract)
                act(Kc("d"), Kc("mq"), F_.Abs)
            xa, ya, ab = ap("ab", 2 * j0, j0 + j1), ap("ab", j0 + j1, 2 * j1), ap("ab", 2 * j0, 2 * j1)
            xr_, yr_, rb = ap("rb", 2 * j0, j0 + j1), ap("rb", j0 + j1, 2 * j1), ap("rb", 2 * j0, 2 * j1)
            xi, yi = ind(ap("xb", b0, b1), sL), ind(ap("dl", b0, b1), sL)
            lead = [(pn, ap("I16"), B16), (pn, ap("In16"), P16), None, (p0, ap("I4"), Kc("lts"))]
            if cfg["LS"][c] == 1:
                gather(xa, xi)
                gather(ya, yi)
                mm([(p0, ap("I"), xa), (p0, ap("In"), Kc("d")), None, (pn, ap("I"), ya), (pn, ap("In"), Kc("d")), (pn, ap("I"), xa)])
                act(rb, ap(kb, 0, 2 * nc), F_.Abs)
                mm(lead + [(p0, ap("BOn"), xr_), (p0, ap("BO"), yr_)])
            else:
                if cfg["LS"][c] == 2:
                    tt(xa, xi, Kc("d"), A_.subtract)
                    tt(ya, yi, xa, A_.add)
                    relu(rb, ab)
                else:
                    gather(xa, xi)
                    tt(ya, yi, xa, A_.add)
                    tt(xr_, xa, Kc("d"), A_.max)
                    tt(yr_, ya, Kc("d"), A_.max)
                mm(lead + [(p0, ap("BO"), xa), (p0, ap("BOn"), ya)], True, False)
                mm([(p0, ap("BOn2"), xr_), (p0, ap("BO2"), yr_)], False, True)
            affine(Kc("dm"), Kc("d"), 1.0, EVEN - 0.5)
            kw = {} if last else {"accum_out": col("ac", 5 if c == nch - 1 else c)}
            act(Kc("m01"), p0, F_.Sign, bias=-0.5, scale=-1.0, **kw)
            if not last and c == nch - 2:
                if c:
                    ts(col("ac", 4), col("ac", 0), col("ac", 1), A_.add, 256.0, A_.add)
                else:
                    affine(col("ac", 4), col("ac", 0), 1.0, 256.0)
            if not last and c == nch - 1:
                mm([(col("p4", 500), ap("W15"), col("ac", 4)), (col("p4", 500), ap("W15"), col("ac", 5))])
            tt(Kc("tz"), pn, Kc("m01"), A_.mult)

            def names(o):
                return [(o, ap("Ih16"), P16), (o, ap("Ih16"), B16), (o, ap("Ih16"), Kc("tz"))]
            mm(names(p0))
            cp(Kc("Z16"), p0)
            where[0] = "c%d%d" % (t, c)
            shared = CC[c] == kb
            p1 = pn if shared else ap(CC[c], 0, nc)
            if not shared:
                mm(names(p1), True, False)
            for (s0, s1) in cuts(j0, cfg["SZ"][c]):
                gather(ap("zb", 16 * s0, 16 * s1), ind(Xw, ap("Z16", s0, s1)))
            for (u0, u1) in pieces(j0, j1, cfg["U2"][c]):
                nu = u1 - u0
                ks = banks(cfg["U2"][c])
                o3, du = ap(kb, u0 - j0, u1 - j0), ap("d", u0, u1)
                nv = cfg["AV"][c]
                mm([(o3, ap("Sh"), ap("lts", u0, u1))] + ([(o3, BK[ks[-nv][0]], du)] if nv else []), True, False)
                for bi, kk in enumerate(ks):
                    bank = ZB[zn[0] % len(ZB)]
                    zn[0] += 1
                    grp = []
                    for i, k in enumerate(kk):
                        o = ap(bank, i * nu, i * nu + nu)
                        grp += [None, (o, ap("I"), ap("zb", 16 * u0 + k, 16 * u1, 16)), (o, ap("In"), du)]
                    mm(grp[1:])
                    ops[-1]["key"] = "pz"
                    az = ap("az", 16 * u0 + kk[0] * nu, 16 * u0 + (kk[-1] + 1) * nu)
                    w = "W"
                    if bi >= len(ks) - nv:
                        mm([(o3, sel("Wn", k), ap("zb", 16 * u0 + k, 16 * u1, 16)) for k in kk], False, False)
                        relu(az, ap(bank, 0, len(kk) * nu))
                        w = "W2"
                    else:
                        act(az, ap(bank, 0, len(kk) * nu), F_.Abs)
                    mm([(o3, sel(w, k), ap("az", 16 * u0 + k * nu, 16 * u0 + k * nu + nu)) for k in kk], False, bi == len(ks) - 1)
            relu(Kc("sg2"), p0, col("bs", 1))
            if shared:
                mm(names(p1) + [(p1, ap("T8n"), Kc("sg2")), None, (p0, ap("T8"), Kc("sg2"))])
            else:
                mm([(p0, ap("T8"), Kc("sg2"))])
                mm([(p1, ap("T8n"), Kc("sg2"))], False, True)
            where[0] = "e%d%d" % (t, c)
            Gc = ap("G", 2 * j0, 2 * j1)
            Go = ind(Gc, ap("cx16", o32 + a0, o32 + a1))
            En = "Eh" if cfg["EP"][c] else "E"
            gf = ap("Gf", 512 * t + 2 * j0, 512 * t + 2 * j1)
            ahead = cfg["EP"][c] and not last
            if ahead:
                send(gf, Gc, t + 2)
                send(ap("clf", 16 * t + a0, 16 * t + a1), ap("cx16", o32 + a0, o32 + a1), t + 2)
            tt(Kc("em"), p0, Kc(En if t else "Ei"), A_.min)
            if cfg["ET"][c] == 2 or last:
                relu(Kc("ea"), p1)
                tt(Go, Kc("ea"), Kc("em"), A_.add)
                if not last:
                    gather(Kc("E"), Go)
            else:
                tt(Kc(En), p1, Kc("em"), A_.max)
                if ahead:
                    ef = ap("Ef", 256 * t + j0, 256 * t + j1)
                    send(ef, Kc(En), t + 2)
                cp(Go, Kc(En))
            if last:
                dma(ap("yl", 2 * j0, 2 * j1), Gc, 1024 * nc)
            elif ahead:
                cp(ind(gf, ap("clf", 16 * t + a0, 16 * t + a1)), ef)
                ops[-1]["key"] = "Gf%d" % c
            else:
                send(gf, Gc, t + 2)
            nought(Kc("lte"), p0)
            tolist(ap(kb, 0, na), "W", "lte", j0, j1, base)
            eL = ap("eL", a0, a1)
            ts(eL, ap(kb, 0, na), -1.0, A_.add)
            tt(Kc("q2"), ind(ap("zb", b0, b1), eL), Kc("dm"), A_.add)
            if last:
                halved(Kc("q"), Kc("q2"))
                dma(ap("yq", j0, j1), Kc("q"), 256 * nc, "S")
        where[0] = "x%d" % t
        parts = pieces(0, C, cfg["SR"])
        for (j0, j1) in parts:
            tt(ap("xo", j0, j1), ind(Xw, ap("cx16", o32 + 16 + j0 // 16, o32 + 16 + j1 // 16)), ap("dm", j0, j1), A_.add)
            halved(ap("x2", j0, j1), ap("xo", j0, j1))
        for (j0, j1) in parts:
            cp(ind(Xn, ap("cx16", o32 + 16 + j0 // 16, o32 + 16 + j1 // 16)), ap("x2", j0, j1))
    dma(ap("yx", 0, 1024), ap("X1", 0, 1024), 262144)
    dma(ap("yx", 1024, 2048), ap("X1", 1024, 2048), 262144)
    return ops


def depend(ops):
    n = len(ops)
    pred = [set() for _ in range(n)]
    hist = {}
    for i, o in enumerate(ops):
        if o["kind"] == "arr":
            pred[i].add(o["x"])
        for (name, lo, hi) in o["rd"]:
            for (j, l2, h2, w) in hist.get(name, []):
                if w and l2 < hi and lo < h2:
                    pred[i].add(j)
        for (name, lo, hi) in o["wr"]:
            keep = []
            for e in hist.get(name, []):
                if e[1] < hi and lo < e[2]:
                    pred[i].add(e[0])
                    if lo <= e[1] and e[2] <= hi:
                        continue
                keep.append(e)
            hist[name] = keep
        for (name, lo, hi) in o["rd"]:
            hist.setdefault(name, []).append((i, lo, hi, False))
        for (name, lo, hi) in o["wr"]:
            hist.setdefault(name, []).append((i, lo, hi, True))
        pred[i].discard(i)
    return pred


def variant(o, e):
    return o if o["eng"] == e else o["alt"]


def classes(ops):
    seen, out = {}, []
    for o in ops:
        g, key = o["grp"], o["key"]
        if o["kind"] == "send" or key[:2] == "cx":
            key = key[:2]
        base, t = key + g[0] + g[2:] + ("" if o["kind"] == "c" else o["kind"][0]), int(g[1:2] or 0)
        k = seen.get((base, t), 0)
        seen[(base, t)] = k + 1
        out.append((base + ("." + str(k) if k else ""), t))
    return out


def timed(ops, pred, table, period):
    tau = {w.split("@")[0].rstrip("*"): (float(w.split("@")[1]), "*" in w) for w in table.split()}
    key, names = [], classes(ops)
    for i, (name, t) in enumerate(names):
        before = [key[j] + 0.00001 for j in pred[i]]
        key.append(max(before + ([tau[name][0] + period * t] if ops[i]["eng"] else [])))
    order = {e: [] for e in "VSPGY"}
    for i in sorted(range(len(ops)), key=lambda i: key[i]):
        if ops[i]["eng"]:
            order["V" if tau[names[i][0]][1] else ops[i]["eng"]].append(i)
    return order


PLAN = []


def rank_program(g, core, T, topo):
    rank = T.rank_of(core)
    if rank is None:
        return
    if not PLAN:
        ops = build(CFG, COST)
        pred = depend(ops)
        PLAN.append((ops, pred, timed(ops, pred, TIMES, PERIOD)))
    ops, pred, order = PLAN[0]
    queue = {"V": g.vector, "S": g.scalar, "P": g.tensor, "G": g, "Y": g.sync}

    def engines(src, dst):
        return len(topo.engines(T.cores[src % N], T.cores[dst % N]))
    done, nm, na = {}, 0, 0
    for e in order:
        k = 0
        for i in order[e]:
            o = ops[i]
            if o["kind"] == "c":
                k += 1
                done[i] = (e, k)
            elif o["kind"] == "dma":
                done[i] = ("m%d" % nm, 16)
                nm += 1
            else:
                done[i] = ("m%d" % nm, engines(rank, rank - o["x"][1]))
                done[i + 1] = ("a%d" % na, engines(rank + o["x"][1], rank))
                nm += 1
                na += 1
    seen_all = {}
    for e in order:
        qu, seen = queue[e], {}
        for i in order[e]:
            o = ops[i]
            need = {}
            for j in pred[i]:
                if e == "P" and ops[j]["eng"] == "P":
                    continue
                s, v = done[j]
                need[s] = max(need.get(s, 0), v)
            for s in sorted(need):
                if seen.get(s, 0) < need[s]:
                    qu.wait_ge(T.sem[s], need[s])
                    seen[s] = need[s]
                    seen_all[s] = max(seen_all.get(s, 0), need[s])
            s, v = done[i]
            if o["kind"] == "send":
                dst = T.cores[(rank - o["x"][1]) % N]
                rid, pid = topo.addr(dst, core)
                g.remote_dma(real(T, o["x"][0]), real(T, o["calls"][0][1][1]), T.sem[done[i + 1][0]], T.sem[s], pid, rid,
                             topo.mask(core, dst))
                continue
            for (m, args, kw) in variant(o, e)["calls"]:
                a = [real(T, x) if is_ap(x) else x for x in args]
                w = {key: (real(T, x) if is_ap(x) else x) for key, x in kw.items()}
                if m == "matmul":
                    ins = qu.matmul(*a)
                elif m == "activation":
                    ins = qu.activation(*a, **w)
                elif m == "iota":
                    ins = qu.iota(*a, **w)
                elif m == "dma_start":
                    ins = qu.dma_start(*a)
                elif m == "memset":
                    ins = qu.memset(*a)
                elif m == "tensor_copy":
                    ins = qu.tensor_copy(*a)
                elif m == "tensor_tensor":
                    ins = qu.tensor_tensor(*a)
                elif m == "tensor_scalar":
                    ins = qu.tensor_scalar(*a)
                else:
                    ins = qu.tensor_tensor_scan(*a)
            ins.then_inc(T.sem[s], 16 if o["kind"] == "dma" else 1)
    total = {}
    for (s, v) in done.values():
        total[s] = max(total.get(s, 0), v)
    for s in sorted(total):
        if seen_all.get(s, 0) < total[s] or s in order:
            g.sync.wait_ge(T.sem[s], total[s])
